import numpy as np
import ml_dtypes


def mxq(x, axis, fmt="e4m3"):
    dtype, down = {"e4m3": (ml_dtypes.float8_e4m3fn, 7), "e5m2": (ml_dtypes.float8_e5m2, 14)}[fmt]
    v = np.moveaxis(np.asarray(x, np.float32).astype(ml_dtypes.bfloat16).astype(np.float64), axis, -1)
    blocks = v.reshape(v.shape[:-1] + (-1, 32))
    amax = np.abs(blocks).max(-1, keepdims=True)
    byte = np.maximum(np.where(amax > 0, np.frexp(amax)[1] - 1 + 127, 0) - down, 1)
    scale = np.exp2(byte - 127.0)
    codes = (blocks / scale).astype(np.float32).astype(dtype).astype(np.float64)
    return np.moveaxis((codes * scale).reshape(v.shape), -1, axis)


WIDE = False


def mx_kscale(k):
    if not WIDE:
        return np.ones(k)
    levels = np.array([10, -10, 5, -5, 0])
    if k % 512:
        return np.exp2(np.random.permutation(np.resize(levels, k // 32))).repeat(32)
    a = np.empty((k // 512, 16))
    for p in range(k // 512):
        a[p, :8] = np.random.permutation(np.resize(levels, 8))
        for g in range(8):
            far = levels[np.abs(levels - a[p, g]) >= 10]
            a[p, g + 8] = far[np.random.randint(len(far))]
    return np.exp2(a.ravel()).repeat(32)


def f64(x):
    return np.asarray(x).astype(np.float64)


def striped(idx):
    return np.tile(idx.reshape(-1, 16).T, (8, 1)).astype(np.uint16)


def unstriped(offs):
    return offs[:16].T.reshape(-1).astype(np.int64)


def pack_weight(w):
    k, n = w.shape
    w = f64(np.asarray(w, np.float32).astype(ml_dtypes.bfloat16)).reshape(k // 32, 32, n)
    amax = np.abs(w).max(1)
    byte = np.clip(np.where(amax > 0, np.frexp(amax)[1] - 1 + 127 - 7, 1), 1, 254)
    scaled = (w * np.exp2(127.0 - byte)[:, None, :]).reshape(k, n).astype(np.float32)
    words = np.ascontiguousarray(scaled.reshape(k // 512, 128, 4, n).transpose(0, 1, 3, 2)).astype(ml_dtypes.float8_e4m3fn).view(np.uint8)
    return words, np.ascontiguousarray(byte.astype(np.uint8).reshape(k // 512, 16, n))


def unpack_weight(words, scales):
    g, p, n, _ = words.shape
    vals = np.ascontiguousarray(words).view(ml_dtypes.float8_e4m3fn).astype(np.float64) * np.repeat(np.exp2(scales.astype(np.float64) - 127.0), 8, axis=1)[..., None]
    return vals.transpose(0, 1, 3, 2).reshape(g * 512, n)


def relu(v):
    return np.maximum(v, 0.0)


def sigmoid(v):
    return 1.0 / (1.0 + np.exp(-np.maximum(v, -700.0)))


K, T, S, N, U = 1024, 1024, 512, 256, 1024


def setup_inputs():
    n = np.random.standard_normal
    s = mx_kscale(K)[:, None]
    packed_w1 = pack_weight(n((K, N)) / np.sqrt(K) / s)
    packed_w2 = pack_weight(n((K, N)) / np.sqrt(K) / s)
    return {
        "xT": (n((K, T)) * s).astype(np.float32),
        "mem": n((N, U)).astype(np.float32),
        "w1_words": packed_w1[0],
        "w1_scales": packed_w1[1],
        "w2_words": packed_w2[0],
        "w2_scales": packed_w2[1],
        "offs": striped(np.random.permutation(T)[:S]),
        "slot": striped(np.random.permutation(U)[:S]),
    }


def reference(xT, mem, w1_words, w1_scales, w2_words, w2_scales, offs, slot):
    old = f64(mem)[:, unstriped(slot)]
    xq = mxq(f64(xT)[:, unstriped(offs)], 0, "e4m3")
    g = sigmoid(unpack_weight(w2_words, w2_scales).T @ xq)
    y = relu(unpack_weight(w1_words, w1_scales).T @ xq)
    out = f64(mem).copy()
    out[:, unstriped(slot)] = old + g * (y - old)
    return out

@@ -1,0 +1,147 @@
+from contextlib import ExitStack
+
+import concourse.mybir as mybir
+
+K, T, S, N, U = 1024, 1024, 512, 256, 1024
+FLOPS = 2 * 2 * K * N * S
+
+F32 = mybir.dt.float32
+BF16 = mybir.dt.bfloat16
+I32 = mybir.dt.int32
+U32 = mybir.dt.uint32
+U16 = mybir.dt.uint16
+U8 = mybir.dt.uint8
+FP8X4 = mybir.dt.float8_e4m3fn_x4
+ALU = mybir.AluOpType
+ACT = mybir.ActivationFunctionType
+
+P = 128
+PACK = 4
+K_PASS = P * PACK
+PASSES = K // K_PASS
+BLOCKS = N // P
+HALF = S // 2
+LANES = 16
+
+CHUNKS = (
+    ((0, 512, 256), (512, 256, 256), (768, 256, 128)),
+    ((0, 256, 256), (256, 512, 256), (768, 256, 128)),
+)
+
+
+def tile_picked_gmem_relu_e_kernel(
+    tc, xT, mem, w1_words, w1_scales, w2_words, w2_scales, offs, slot, out
+):
+    nc = tc.nc
+    with ExitStack() as ctx:
+        keep = ctx.enter_context(tc.tile_pool(name="keep", bufs=1))
+        psum = ctx.enter_context(tc.psum_pool(name="psum", bufs=1))
+
+        offs_sb = keep.tile([P, S // LANES], U16, name="offs_sb")
+        slot_sb = keep.tile([P, S // LANES], U16, name="slot_sb")
+
+        raw = {}
+        for z in range(PASSES):
+            rows = xT[z * K_PASS : (z + 1) * K_PASS, :].rearrange("(p j) t -> p j t", j=PACK)
+            for c0, width, share in CHUNKS[z]:
+                raw[z, c0] = keep.tile([P, PACK, width], F32, name=f"raw{z}_{c0}")
+                nc.sync.dma_start(out=raw[z, c0][:], in_=rows[:, :, c0 : c0 + width])
+            if z == 0:
+                nc.sync.dma_start(offs_sb[:], offs)
+
+        w_scales = keep.tile([P, 2 * N], U8, name="w_scales", align_bytes=64)
+        nc.gpsimd.memset(w_scales[:].bitcast(I32), 0)
+        for i, scales, queue in ((1, w2_scales, nc.gpsimd), (0, w1_scales, nc.sync)):
+            for q in range(4):
+                queue.dma_start(
+                    out=w_scales[32 * q : 32 * q + 4 * PASSES, i * N : (i + 1) * N].bitcast(I32),
+                    in_=scales[:, 4 * q : 4 * q + 4, :].bitcast(I32),
+                )
+
+        w_words = []
+        for i, words in enumerate((w1_words, w2_words)):
+            tile = keep.tile([P, PASSES, N], U32, name=f"w_words{i}", align_bytes=64)
+            nc.sync.dma_start(
+                out=tile[:].bitcast(I32), in_=words.rearrange("z p n r -> p z (n r)").bitcast(I32)
+            )
+            w_words.append(tile)
+        memory = []
+        for b in range(BLOCKS):
+            tile = keep.tile([P, U], F32, name=f"memory{b}")
+            nc.sync.dma_start(out=tile[:], in_=mem[b * P : (b + 1) * P, :])
+            memory.append(tile)
+            if b == 0:
+                nc.sync.dma_start(slot_sb[:], slot)
+
+        def interleave(copy, source, c0, width, name):
+            grouped = keep.tile([P, width, PACK], BF16, name=name, align_bytes=64)
+            copy(
+                grouped[:].rearrange("p (c i) j -> p c j i", i=4),
+                source[:, :, c0 : c0 + width].rearrange("p j (c i) -> p c j i", i=4),
+            )
+            return grouped
+
+        def scalar_copy(dst, src):
+            nc.scalar.activation(dst, src, ACT.Copy)
+
+        acc = {}
+        for z in range(PASSES):
+            x_words = keep.tile([P, T], U32, name=f"x_words{z}", align_bytes=64)
+            x_bytes = keep.tile([P, T], U8, name=f"x_bytes{z}", align_bytes=64)
+            nc.vector.memset(x_bytes[:].bitcast(I32), 0)
+            for c0, width, share in CHUNKS[z]:
+                parts = [(0, share, scalar_copy)]
+                if share < width:
+                    parts = [(share, width - share, nc.vector.tensor_copy)] + parts
+                made = [
+                    (c0 + a, w, interleave(copy, raw[z, c0], a, w, f"grouped{z}_{c0 + a}"))
+                    for a, w, copy in parts
+                ]
+                for a, w, grouped in made:
+                    nc.vector.quantize_mx(
+                        out=x_words[:, a : a + w].bitcast(FP8X4),
+                        scales=x_bytes[:, a : a + w],
+                        in_=grouped[:].rearrange("p c j -> p (c j)"),
+                    )
+            pieces = [(0, S)] if z == 0 else [(0, HALF), (HALF, HALF)]
+            for s0, count in pieces:
+                picks = offs_sb[:, s0 // LANES : (s0 + count) // LANES]
+                g_words = keep.tile([P, count], U32, name=f"g_words{z}_{s0}", align_bytes=64)
+                g_bytes = keep.tile([P, count], U8, name=f"g_bytes{z}_{s0}", align_bytes=64)
+                nc.vector.tensor_copy(g_words[:], x_words[:].indirect(picks))
+                nc.vector.tensor_copy(g_bytes[:], x_bytes[:].indirect(picks))
+                for h0 in range(s0, s0 + count, HALF):
+                    cols = slice(h0 - s0, h0 - s0 + HALF)
+                    for b in range(BLOCKS):
+                        for i in (1, 0):
+                            if z == 0:
+                                acc[i, b, h0] = psum.tile([P, HALF], F32, name=f"acc{i}_{b}_{h0}")
+                            nc.tensor.matmul_mx(
+                                out=acc[i, b, h0][:],
+                                lhsT=w_words[i][:, z, b * P : (b + 1) * P].bitcast(FP8X4),
+                                lhsT_scale=w_scales[4 * z : P, i * N + b * P : i * N + (b + 1) * P],
+                                rhs=g_words[:, cols].bitcast(FP8X4),
+                                rhs_scale=g_bytes[:, cols],
+                                start=(z == 0),
+                                stop=(z == PASSES - 1),
+                            )
+
+        for b in range(BLOCKS):
+            gate = keep.tile([P, S], F32, name=f"gate{b}")
+            rest = keep.tile([P, S], F32, name=f"rest{b}")
+            fresh = keep.tile([P, S], F32, name=f"fresh{b}")
+            kept = keep.tile([P, S], F32, name=f"kept{b}")
+            for h0 in range(0, S, HALF):
+                cols = slice(h0, h0 + HALF)
+                nc.scalar.activation(gate[:, cols], acc[1, b, h0][:], ACT.Sigmoid)
+                nc.scalar.activation(rest[:, cols], acc[1, b, h0][:], ACT.Sigmoid, scale=-1.0)
+                nc.vector.scalar_tensor_tensor(
+                    fresh[:, cols], acc[0, b, h0][:], 0.0, gate[:, cols], ALU.max, ALU.mult
+                )
+                if b == 0:
+                    places = slot_sb[:, h0 // LANES : (h0 + HALF) // LANES]
+                    nc.vector.tensor_tensor(kept[:, cols], memory[b][:].indirect(places), rest[:, cols], ALU.mult)
+            if b > 0:
+                nc.vector.tensor_tensor(kept[:], memory[b][:].indirect(slot_sb[:]), rest[:], ALU.mult)
+            nc.vector.tensor_tensor(memory[b][:].indirect(slot_sb[:]), fresh[:], kept[:], ALU.add)
+            nc.sync.dma_start(out=out[b * P : (b + 1) * P, :], in_=memory[b][:])

@@ -22,10 +22,11 @@ PASSES = K // K_PASS
 BLOCKS = N // P
 HALF = S // 2
 LANES = 16
+GATE, CANDIDATE = 0, 1
 
 CHUNKS = (
+    ((0, 512, 256), (512, 512, 256)),
     ((0, 512, 256), (512, 256, 256), (768, 256, 128)),
-    ((0, 256, 256), (256, 512, 256), (768, 256, 128)),
 )
 
 
@@ -40,6 +41,9 @@ def tile_picked_gmem_relu_e_kernel(
         offs_sb = keep.tile([P, S // LANES], U16, name="offs_sb")
         slot_sb = keep.tile([P, S // LANES], U16, name="slot_sb")
 
+        def entries(table, first, count):
+            return table[:, first // LANES : (first + count) // LANES]
+
         raw = {}
         for z in range(PASSES):
             rows = xT[z * K_PASS : (z + 1) * K_PASS, :].rearrange("(p j) t -> p j t", j=PACK)
@@ -48,30 +52,23 @@ def tile_picked_gmem_relu_e_kernel(
                 nc.sync.dma_start(out=raw[z, c0][:], in_=rows[:, :, c0 : c0 + width])
             if z == 0:
                 nc.sync.dma_start(offs_sb[:], offs)
+                nc.sync.dma_start(slot_sb[:], slot)
 
         w_scales = keep.tile([P, 2 * N], U8, name="w_scales", align_bytes=64)
-        nc.gpsimd.memset(w_scales[:].bitcast(I32), 0)
-        for i, scales, queue in ((1, w2_scales, nc.gpsimd), (0, w1_scales, nc.sync)):
+        for i, scales, queue in ((GATE, w2_scales, nc.gpsimd), (CANDIDATE, w1_scales, nc.sync)):
             for q in range(4):
                 queue.dma_start(
                     out=w_scales[32 * q : 32 * q + 4 * PASSES, i * N : (i + 1) * N].bitcast(I32),
                     in_=scales[:, 4 * q : 4 * q + 4, :].bitcast(I32),
                 )
-
+        memory = [keep.tile([P, U], F32, name=f"memory{b}") for b in range(N // P)]
+        nc.sync.dma_start(out=memory[0][:], in_=mem[0:P, :])
         w_words = []
-        for i, words in enumerate((w1_words, w2_words)):
+        for i, words in ((GATE, w2_words), (CANDIDATE, w1_words)):
             tile = keep.tile([P, PASSES, N], U32, name=f"w_words{i}", align_bytes=64)
-            nc.sync.dma_start(
-                out=tile[:].bitcast(I32), in_=words.rearrange("z p n r -> p z (n r)").bitcast(I32)
-            )
+            nc.sync.dma_start(out=tile[:].bitcast(I32), in_=words.rearrange("z p n r -> p z (n r)").bitcast(I32))
             w_words.append(tile)
-        memory = []
-        for b in range(BLOCKS):
-            tile = keep.tile([P, U], F32, name=f"memory{b}")
-            nc.sync.dma_start(out=tile[:], in_=mem[b * P : (b + 1) * P, :])
-            memory.append(tile)
-            if b == 0:
-                nc.sync.dma_start(slot_sb[:], slot)
+        nc.sync.dma_start(out=memory[1][:], in_=mem[P : 2 * P, :])
 
         def interleave(copy, source, c0, width, name):
             grouped = keep.tile([P, width, PACK], BF16, name=name, align_bytes=64)
@@ -84,11 +81,12 @@ def tile_picked_gmem_relu_e_kernel(
         def scalar_copy(dst, src):
             nc.scalar.activation(dst, src, ACT.Copy)
 
-        acc = {}
+        x_bytes = keep.tile([P, T], U8, name="x_bytes", align_bytes=64)
+        nc.vector.memset(x_bytes[:].bitcast(I32), 0)
+        g_bytes = keep.tile([P, S], U8, name="g_bytes", align_bytes=64)
+        g_words = []
         for z in range(PASSES):
-            x_words = keep.tile([P, T], U32, name=f"x_words{z}", align_bytes=64)
-            x_bytes = keep.tile([P, T], U8, name=f"x_bytes{z}", align_bytes=64)
-            nc.vector.memset(x_bytes[:].bitcast(I32), 0)
+            x_words = keep.tile([P, T], U32, name=f"x_words{z}", tag=f"x_words{z}", align_bytes=64)
             for c0, width, share in CHUNKS[z]:
                 parts = [(0, share, scalar_copy)]
                 if share < width:
@@ -100,48 +98,76 @@ def tile_picked_gmem_relu_e_kernel(
                 for a, w, grouped in made:
                     nc.vector.quantize_mx(
                         out=x_words[:, a : a + w].bitcast(FP8X4),
-                        scales=x_bytes[:, a : a + w],
+                        scales=x_bytes[4 * z : P, a : a + w],
                         in_=grouped[:].rearrange("p c j -> p (c j)"),
                     )
-            pieces = [(0, S)] if z == 0 else [(0, HALF), (HALF, HALF)]
-            for s0, count in pieces:
-                picks = offs_sb[:, s0 // LANES : (s0 + count) // LANES]
-                g_words = keep.tile([P, count], U32, name=f"g_words{z}_{s0}", align_bytes=64)
-                g_bytes = keep.tile([P, count], U8, name=f"g_bytes{z}_{s0}", align_bytes=64)
-                nc.vector.tensor_copy(g_words[:], x_words[:].indirect(picks))
-                nc.vector.tensor_copy(g_bytes[:], x_bytes[:].indirect(picks))
-                for h0 in range(s0, s0 + count, HALF):
-                    cols = slice(h0 - s0, h0 - s0 + HALF)
-                    for b in range(BLOCKS):
-                        for i in (1, 0):
-                            if z == 0:
-                                acc[i, b, h0] = psum.tile([P, HALF], F32, name=f"acc{i}_{b}_{h0}")
-                            nc.tensor.matmul_mx(
-                                out=acc[i, b, h0][:],
-                                lhsT=w_words[i][:, z, b * P : (b + 1) * P].bitcast(FP8X4),
-                                lhsT_scale=w_scales[4 * z : P, i * N + b * P : i * N + (b + 1) * P],
-                                rhs=g_words[:, cols].bitcast(FP8X4),
-                                rhs_scale=g_bytes[:, cols],
-                                start=(z == 0),
-                                stop=(z == PASSES - 1),
-                            )
+            picked = keep.tile([P, S], U32, name=f"g_words{z}", align_bytes=64)
+            g_words.append(picked)
+            if z < PASSES - 1:
+                nc.vector.tensor_copy(picked[:], x_words[:].indirect(offs_sb[:]))
+            else:
+                for h0 in range(0, S, HALF):
+                    picks = offs_sb[:, h0 // LANES : (h0 + HALF) // LANES]
+                    nc.vector.tensor_copy(picked[:, h0 : h0 + HALF], x_words[:].indirect(picks))
+                    nc.vector.tensor_copy(g_bytes[:, h0 : h0 + HALF], x_bytes[:].indirect(picks))
 
-        for b in range(BLOCKS):
-            gate = keep.tile([P, S], F32, name=f"gate{b}")
-            rest = keep.tile([P, S], F32, name=f"rest{b}")
-            fresh = keep.tile([P, S], F32, name=f"fresh{b}")
-            kept = keep.tile([P, S], F32, name=f"kept{b}")
-            for h0 in range(0, S, HALF):
-                cols = slice(h0, h0 + HALF)
-                nc.scalar.activation(gate[:, cols], acc[1, b, h0][:], ACT.Sigmoid)
-                nc.scalar.activation(rest[:, cols], acc[1, b, h0][:], ACT.Sigmoid, scale=-1.0)
-                nc.vector.scalar_tensor_tensor(
-                    fresh[:, cols], acc[0, b, h0][:], 0.0, gate[:, cols], ALU.max, ALU.mult
-                )
-                if b == 0:
-                    places = slot_sb[:, h0 // LANES : (h0 + HALF) // LANES]
-                    nc.vector.tensor_tensor(kept[:, cols], memory[b][:].indirect(places), rest[:, cols], ALU.mult)
-            if b > 0:
-                nc.vector.tensor_tensor(kept[:], memory[b][:].indirect(slot_sb[:]), rest[:], ALU.mult)
-            nc.vector.tensor_tensor(memory[b][:].indirect(slot_sb[:]), fresh[:], kept[:], ALU.add)
-            nc.sync.dma_start(out=out[b * P : (b + 1) * P, :], in_=memory[b][:])
+        pieces = ((0, 0, HALF), (0, HALF, HALF), (1, 0, S))
+        acc = {}
+        for piece in pieces:
+            b, s0, count = piece
+            for i in (GATE, CANDIDATE):
+                acc[i, piece] = psum.tile([P, count], F32, name=f"acc{i}_{b}_{s0}")
+                for z in range(PASSES):
+                    nc.tensor.matmul_mx(
+                        out=acc[i, piece][:],
+                        lhsT=w_words[i][:, z, b * P : (b + 1) * P].bitcast(FP8X4),
+                        lhsT_scale=w_scales[4 * z : P, i * N + b * P : i * N + (b + 1) * P],
+                        rhs=g_words[z][:, s0 : s0 + count].bitcast(FP8X4),
+                        rhs_scale=g_bytes[4 * z : P, s0 : s0 + count],
+                        start=(z == 0),
+                        stop=(z == PASSES - 1),
+                    )
+
+        gate, rest, kept, fresh = {}, {}, {}, {}
+        for piece in pieces:
+            b, s0, count = piece
+            for table, name in ((gate, "gate"), (rest, "rest"), (kept, "kept")):
+                table[piece] = keep.tile([P, count], F32, name=f"{name}{b}_{s0}")
+        first, second, third = pieces
+        fresh[first] = keep.tile([P, HALF], F32, name="fresh_first")[:]
+        fresh[third] = keep.tile([P, S], F32, name="fresh_third")[:]
+        fresh[second] = gate[third][:, :HALF]
+
+        def sigmoid(piece, table, sign):
+            nc.scalar.activation(table[piece][:], acc[GATE, piece][:], ACT.Sigmoid, scale=sign)
+
+        def gated_candidate(piece):
+            nc.vector.scalar_tensor_tensor(
+                fresh[piece], acc[CANDIDATE, piece][:], 0.0, gate[piece][:], ALU.max, ALU.mult
+            )
+
+        def put_back(piece):
+            b, s0, count = piece
+            nc.vector.tensor_tensor(
+                memory[b][:].indirect(entries(slot_sb, s0, count)), fresh[piece], kept[piece][:], ALU.add
+            )
+
+        old = keep.tile([P, S], F32, name="old", tag="x_words1", align_bytes=64)
+        nc.vector.tensor_copy(old[:], memory[0][:].indirect(slot_sb[:]))
+        for piece in (first, second):
+            sigmoid(piece, rest, -1.0)
+            sigmoid(piece, gate, 1.0)
+        sigmoid(third, gate, 1.0)
+        sigmoid(third, rest, -1.0)
+
+        nc.vector.tensor_tensor(kept[first][:], old[:, :HALF], rest[first][:], ALU.mult)
+        gated_candidate(first)
+        nc.vector.tensor_tensor(kept[second][:], old[:, HALF:], rest[second][:], ALU.mult)
+        put_back(first)
+        gated_candidate(third)
+        nc.vector.tensor_tensor(kept[third][:], memory[1][:].indirect(slot_sb[:]), rest[third][:], ALU.mult)
+        gated_candidate(second)
+        put_back(third)
+        nc.sync.dma_start(out=out[P : 2 * P, :], in_=memory[1][:])
+        put_back(second)
+        nc.sync.dma_start(out=out[0:P, :], in_=memory[0][:])

@@ -19,14 +19,16 @@ P = 128
 PACK = 4
 K_PASS = P * PACK
 PASSES = K // K_PASS
-BLOCKS = N // P
-HALF = S // 2
+QUADRANT = 32
+SCALE_ROWS = 4
+LINE = 4
 LANES = 16
+HALF = S // 2
 GATE, CANDIDATE = 0, 1
 
 CHUNKS = (
-    ((0, 512, 256), (512, 512, 256)),
-    ((0, 512, 256), (512, 256, 256), (768, 256, 128)),
+    ((256, 256), (256, 256)),
+    ((256, 256), (0, 256), (128, 128)),
 )
 
 
@@ -41,75 +43,84 @@ def tile_picked_gmem_relu_e_kernel(
         offs_sb = keep.tile([P, S // LANES], U16, name="offs_sb")
         slot_sb = keep.tile([P, S // LANES], U16, name="slot_sb")
 
-        def entries(table, first, count):
-            return table[:, first // LANES : (first + count) // LANES]
+        def entries(list_tile, first, count):
+            return list_tile[:, first // LANES : (first + count) // LANES]
 
         raw = {}
         for z in range(PASSES):
             rows = xT[z * K_PASS : (z + 1) * K_PASS, :].rearrange("(p j) t -> p j t", j=PACK)
-            for c0, width, share in CHUNKS[z]:
-                raw[z, c0] = keep.tile([P, PACK, width], F32, name=f"raw{z}_{c0}")
-                nc.sync.dma_start(out=raw[z, c0][:], in_=rows[:, :, c0 : c0 + width])
+            c0 = 0
+            for n, shares in enumerate(CHUNKS[z]):
+                width = sum(shares)
+                raw[z, n] = keep.tile([P, PACK, width], F32, name=f"raw{z}_{n}")
+                nc.sync.dma_start(out=raw[z, n][:], in_=rows[:, :, c0 : c0 + width])
+                c0 = c0 + width
             if z == 0:
                 nc.sync.dma_start(offs_sb[:], offs)
                 nc.sync.dma_start(slot_sb[:], slot)
 
         w_scales = keep.tile([P, 2 * N], U8, name="w_scales", align_bytes=64)
         for i, scales, queue in ((GATE, w2_scales, nc.gpsimd), (CANDIDATE, w1_scales, nc.sync)):
-            for q in range(4):
+            for q in range(P // QUADRANT):
+                live_rows = slice(QUADRANT * q, QUADRANT * q + SCALE_ROWS * PASSES)
                 queue.dma_start(
-                    out=w_scales[32 * q : 32 * q + 4 * PASSES, i * N : (i + 1) * N].bitcast(I32),
-                    in_=scales[:, 4 * q : 4 * q + 4, :].bitcast(I32),
+                    out=w_scales[live_rows, i * N : (i + 1) * N].bitcast(I32),
+                    in_=scales[:, SCALE_ROWS * q : SCALE_ROWS * (q + 1), :].bitcast(I32),
                 )
+
         memory = [keep.tile([P, U], F32, name=f"memory{b}") for b in range(N // P)]
         nc.sync.dma_start(out=memory[0][:], in_=mem[0:P, :])
-        w_words = []
-        for i, words in ((GATE, w2_words), (CANDIDATE, w1_words)):
-            tile = keep.tile([P, PASSES, N], U32, name=f"w_words{i}", align_bytes=64)
-            nc.sync.dma_start(out=tile[:].bitcast(I32), in_=words.rearrange("z p n r -> p z (n r)").bitcast(I32))
-            w_words.append(tile)
+        w_words = {}
+        for b in range(N // P):
+            for i, words in ((GATE, w2_words), (CANDIDATE, w1_words)):
+                w_words[i, b] = keep.tile([P, PASSES, P], U32, name=f"w_words{i}_{b}", align_bytes=64)
+                columns = words[:, :, b * P : (b + 1) * P, :].rearrange("z p n r -> p z (n r)")
+                nc.sync.dma_start(out=w_words[i, b][:].bitcast(I32), in_=columns.bitcast(I32))
         nc.sync.dma_start(out=memory[1][:], in_=mem[P : 2 * P, :])
-
-        def interleave(copy, source, c0, width, name):
-            grouped = keep.tile([P, width, PACK], BF16, name=name, align_bytes=64)
-            copy(
-                grouped[:].rearrange("p (c i) j -> p c j i", i=4),
-                source[:, :, c0 : c0 + width].rearrange("p j (c i) -> p c j i", i=4),
-            )
-            return grouped
 
         def scalar_copy(dst, src):
             nc.scalar.activation(dst, src, ACT.Copy)
 
+        def interleave(copy, source, name):
+            grouped = keep.tile([P, source.shape[2], PACK], BF16, name=name, align_bytes=64)
+            copy(
+                grouped[:].rearrange("p (c i) j -> p c j i", i=LINE),
+                source.rearrange("p j (c i) -> p c j i", i=LINE),
+            )
+            return grouped
+
         x_bytes = keep.tile([P, T], U8, name="x_bytes", align_bytes=64)
         nc.vector.memset(x_bytes[:].bitcast(I32), 0)
-        g_bytes = keep.tile([P, S], U8, name="g_bytes", align_bytes=64)
-        g_words = []
+        picked_bytes = keep.tile([P, S], U8, name="picked_bytes", align_bytes=64)
+        picked_words = []
         for z in range(PASSES):
             x_words = keep.tile([P, T], U32, name=f"x_words{z}", tag=f"x_words{z}", align_bytes=64)
-            for c0, width, share in CHUNKS[z]:
-                parts = [(0, share, scalar_copy)]
-                if share < width:
-                    parts = [(share, width - share, nc.vector.tensor_copy)] + parts
-                made = [
-                    (c0 + a, w, interleave(copy, raw[z, c0], a, w, f"grouped{z}_{c0 + a}"))
-                    for a, w, copy in parts
-                ]
-                for a, w, grouped in made:
+            c0 = 0
+            for n, shares in enumerate(CHUNKS[z]):
+                rounded = []
+                first = 0
+                for width, copy in zip(shares, (nc.vector.tensor_copy, scalar_copy)):
+                    if width > 0:
+                        source = raw[z, n][:, :, first : first + width]
+                        rounded.append(interleave(copy, source, f"grouped{z}_{c0 + first}"))
+                        first = first + width
+                for grouped in rounded:
+                    width = grouped.shape[1]
                     nc.vector.quantize_mx(
-                        out=x_words[:, a : a + w].bitcast(FP8X4),
-                        scales=x_bytes[4 * z : P, a : a + w],
+                        out=x_words[:, c0 : c0 + width].bitcast(FP8X4),
+                        scales=x_bytes[SCALE_ROWS * z : P, c0 : c0 + width],
                         in_=grouped[:].rearrange("p c j -> p (c j)"),
                     )
-            picked = keep.tile([P, S], U32, name=f"g_words{z}", align_bytes=64)
-            g_words.append(picked)
+                    c0 = c0 + width
+            picked = keep.tile([P, S], U32, name=f"picked_words{z}", align_bytes=64)
+            picked_words.append(picked)
             if z < PASSES - 1:
                 nc.vector.tensor_copy(picked[:], x_words[:].indirect(offs_sb[:]))
             else:
-                for h0 in range(0, S, HALF):
-                    picks = offs_sb[:, h0 // LANES : (h0 + HALF) // LANES]
-                    nc.vector.tensor_copy(picked[:, h0 : h0 + HALF], x_words[:].indirect(picks))
-                    nc.vector.tensor_copy(g_bytes[:, h0 : h0 + HALF], x_bytes[:].indirect(picks))
+                for s0 in range(0, S, HALF):
+                    picks = entries(offs_sb, s0, HALF)
+                    nc.vector.tensor_copy(picked[:, s0 : s0 + HALF], x_words[:].indirect(picks))
+                    nc.vector.tensor_copy(picked_bytes[:, s0 : s0 + HALF], x_bytes[:].indirect(picks))
 
         pieces = ((0, 0, HALF), (0, HALF, HALF), (1, 0, S))
         acc = {}
@@ -120,10 +131,10 @@ def tile_picked_gmem_relu_e_kernel(
                 for z in range(PASSES):
                     nc.tensor.matmul_mx(
                         out=acc[i, piece][:],
-                        lhsT=w_words[i][:, z, b * P : (b + 1) * P].bitcast(FP8X4),
-                        lhsT_scale=w_scales[4 * z : P, i * N + b * P : i * N + (b + 1) * P],
-                        rhs=g_words[z][:, s0 : s0 + count].bitcast(FP8X4),
-                        rhs_scale=g_bytes[4 * z : P, s0 : s0 + count],
+                        lhsT=w_words[i, b][:, z, :].bitcast(FP8X4),
+                        lhsT_scale=w_scales[SCALE_ROWS * z : P, i * N + b * P : i * N + (b + 1) * P],
+                        rhs=picked_words[z][:, s0 : s0 + count].bitcast(FP8X4),
+                        rhs_scale=picked_bytes[SCALE_ROWS * z : P, s0 : s0 + count],
                         start=(z == 0),
                         stop=(z == PASSES - 1),
                     )
@@ -131,15 +142,15 @@ def tile_picked_gmem_relu_e_kernel(
         gate, rest, kept, fresh = {}, {}, {}, {}
         for piece in pieces:
             b, s0, count = piece
-            for table, name in ((gate, "gate"), (rest, "rest"), (kept, "kept")):
-                table[piece] = keep.tile([P, count], F32, name=f"{name}{b}_{s0}")
-        first, second, third = pieces
-        fresh[first] = keep.tile([P, HALF], F32, name="fresh_first")[:]
-        fresh[third] = keep.tile([P, S], F32, name="fresh_third")[:]
-        fresh[second] = gate[third][:, :HALF]
+            for tiles, name in ((gate, "gate"), (rest, "rest"), (kept, "kept")):
+                tiles[piece] = keep.tile([P, count], F32, name=f"{name}{b}_{s0}")
+        early, late, whole = pieces
+        fresh[early] = keep.tile([P, HALF], F32, name="fresh_early")[:]
+        fresh[whole] = keep.tile([P, S], F32, name="fresh_whole")[:]
+        fresh[late] = gate[whole][:, :HALF]
 
-        def sigmoid(piece, table, sign):
-            nc.scalar.activation(table[piece][:], acc[GATE, piece][:], ACT.Sigmoid, scale=sign)
+        def sigmoid(piece, tiles, sign):
+            nc.scalar.activation(tiles[piece][:], acc[GATE, piece][:], ACT.Sigmoid, scale=sign)
 
         def gated_candidate(piece):
             nc.vector.scalar_tensor_tensor(
@@ -152,22 +163,22 @@ def tile_picked_gmem_relu_e_kernel(
                 memory[b][:].indirect(entries(slot_sb, s0, count)), fresh[piece], kept[piece][:], ALU.add
             )
 
-        old = keep.tile([P, S], F32, name="old", tag="x_words1", align_bytes=64)
+        old = keep.tile([P, S], F32, name="old", tag=f"x_words{PASSES - 1}", align_bytes=64)
         nc.vector.tensor_copy(old[:], memory[0][:].indirect(slot_sb[:]))
-        for piece in (first, second):
+        for piece in (early, late):
             sigmoid(piece, rest, -1.0)
             sigmoid(piece, gate, 1.0)
-        sigmoid(third, gate, 1.0)
-        sigmoid(third, rest, -1.0)
+        sigmoid(whole, gate, 1.0)
+        sigmoid(whole, rest, -1.0)
 
-        nc.vector.tensor_tensor(kept[first][:], old[:, :HALF], rest[first][:], ALU.mult)
-        gated_candidate(first)
-        nc.vector.tensor_tensor(kept[second][:], old[:, HALF:], rest[second][:], ALU.mult)
-        put_back(first)
-        gated_candidate(third)
-        nc.vector.tensor_tensor(kept[third][:], memory[1][:].indirect(slot_sb[:]), rest[third][:], ALU.mult)
-        gated_candidate(second)
-        put_back(third)
+        nc.vector.tensor_tensor(kept[early][:], old[:, :HALF], rest[early][:], ALU.mult)
+        gated_candidate(early)
+        nc.vector.tensor_tensor(kept[late][:], old[:, HALF:], rest[late][:], ALU.mult)
+        put_back(early)
+        gated_candidate(whole)
+        nc.vector.tensor_tensor(kept[whole][:], memory[1][:].indirect(slot_sb[:]), rest[whole][:], ALU.mult)
+        gated_candidate(late)
+        put_back(whole)
         nc.sync.dma_start(out=out[P : 2 * P, :], in_=memory[1][:])
-        put_back(second)
+        put_back(late)
         nc.sync.dma_start(out=out[0:P, :], in_=memory[0][:])

@@ -27,8 +27,8 @@ HALF = S // 2
 GATE, CANDIDATE = 0, 1
 
 CHUNKS = (
-    ((256, 256), (256, 256)),
-    ((256, 256), (0, 256), (128, 128)),
+    ((256, 256), (160, 96), (160, 96)),
+    ((0, 256), (128, 128), (128, 128), (0, 128), (128, 0)),
 )
 
 
@@ -81,13 +81,11 @@ def tile_picked_gmem_relu_e_kernel(
         def scalar_copy(dst, src):
             nc.scalar.activation(dst, src, ACT.Copy)
 
-        def interleave(copy, source, name):
-            grouped = keep.tile([P, source.shape[2], PACK], BF16, name=name, align_bytes=64)
+        def interleave(copy, grouped, source):
             copy(
-                grouped[:].rearrange("p (c i) j -> p c j i", i=LINE),
+                grouped.rearrange("p (c i) j -> p c j i", i=LINE),
                 source.rearrange("p j (c i) -> p c j i", i=LINE),
             )
-            return grouped
 
         x_bytes = keep.tile([P, T], U8, name="x_bytes", align_bytes=64)
         nc.vector.memset(x_bytes[:].bitcast(I32), 0)
@@ -97,21 +95,20 @@ def tile_picked_gmem_relu_e_kernel(
             x_words = keep.tile([P, T], U32, name=f"x_words{z}", tag=f"x_words{z}", align_bytes=64)
             c0 = 0
             for n, shares in enumerate(CHUNKS[z]):
-                rounded = []
+                width = sum(shares)
+                grouped = keep.tile([P, width, PACK], BF16, name=f"grouped{z}_{n}", align_bytes=64)
                 first = 0
-                for width, copy in zip(shares, (nc.vector.tensor_copy, scalar_copy)):
-                    if width > 0:
-                        source = raw[z, n][:, :, first : first + width]
-                        rounded.append(interleave(copy, source, f"grouped{z}_{c0 + first}"))
-                        first = first + width
-                for grouped in rounded:
-                    width = grouped.shape[1]
-                    nc.vector.quantize_mx(
-                        out=x_words[:, c0 : c0 + width].bitcast(FP8X4),
-                        scales=x_bytes[SCALE_ROWS * z : P, c0 : c0 + width],
-                        in_=grouped[:].rearrange("p c j -> p (c j)"),
-                    )
-                    c0 = c0 + width
+                for share, copy in zip(shares, (nc.vector.tensor_copy, scalar_copy)):
+                    if share > 0:
+                        cols = slice(first, first + share)
+                        interleave(copy, grouped[:, cols, :], raw[z, n][:, :, cols])
+                        first = first + share
+                nc.vector.quantize_mx(
+                    out=x_words[:, c0 : c0 + width].bitcast(FP8X4),
+                    scales=x_bytes[SCALE_ROWS * z : P, c0 : c0 + width],
+                    in_=grouped[:].rearrange("p c j -> p (c j)"),
+                )
+                c0 = c0 + width
             picked = keep.tile([P, S], U32, name=f"picked_words{z}", align_bytes=64)
             picked_words.append(picked)
             if z < PASSES - 1:

@@ -27,8 +27,8 @@ HALF = S // 2
 GATE, CANDIDATE = 0, 1
 
 CHUNKS = (
-    ((256, 256), (160, 96), (160, 96)),
-    ((0, 256), (128, 128), (128, 128), (0, 128), (128, 0)),
+    ((256, 256), (64, 192), (160, 96)),
+    ((0, 256), (0, 256), (128, 128), (32, 96), (80, 48)),
 )
 
 
@@ -120,28 +120,34 @@ def tile_picked_gmem_relu_e_kernel(
                     nc.vector.tensor_copy(picked_bytes[:, s0 : s0 + HALF], x_bytes[:].indirect(picks))
 
         pieces = ((0, 0, HALF), (0, HALF, HALF), (1, 0, S))
+        early, late, whole = pieces
         acc = {}
-        for piece in pieces:
+
+        def product(i, piece, bank):
             b, s0, count = piece
-            for i in (GATE, CANDIDATE):
-                acc[i, piece] = psum.tile([P, count], F32, name=f"acc{i}_{b}_{s0}")
-                for z in range(PASSES):
-                    nc.tensor.matmul_mx(
-                        out=acc[i, piece][:],
-                        lhsT=w_words[i, b][:, z, :].bitcast(FP8X4),
-                        lhsT_scale=w_scales[SCALE_ROWS * z : P, i * N + b * P : i * N + (b + 1) * P],
-                        rhs=picked_words[z][:, s0 : s0 + count].bitcast(FP8X4),
-                        rhs_scale=picked_bytes[SCALE_ROWS * z : P, s0 : s0 + count],
-                        start=(z == 0),
-                        stop=(z == PASSES - 1),
-                    )
+            acc[i, piece] = psum.tile([P, count], F32, name=f"acc{i}_{b}_{s0}", tag=bank)
+            for z in range(PASSES):
+                nc.tensor.matmul_mx(
+                    out=acc[i, piece][:],
+                    lhsT=w_words[i, b][:, z, :].bitcast(FP8X4),
+                    lhsT_scale=w_scales[SCALE_ROWS * z : P, i * N + b * P : i * N + (b + 1) * P],
+                    rhs=picked_words[z][:, s0 : s0 + count].bitcast(FP8X4),
+                    rhs_scale=picked_bytes[SCALE_ROWS * z : P, s0 : s0 + count],
+                    start=(z == 0),
+                    stop=(z == PASSES - 1),
+                )
+
+        product(GATE, early, "gate_early")
+        product(CANDIDATE, early, "candidate_early")
+        product(GATE, late, "gate_late")
+        product(GATE, whole, "gate_whole")
+        product(CANDIDATE, whole, "candidate_whole")
 
         gate, rest, kept, fresh = {}, {}, {}, {}
         for piece in pieces:
             b, s0, count = piece
             for tiles, name in ((gate, "gate"), (rest, "rest"), (kept, "kept")):
                 tiles[piece] = keep.tile([P, count], F32, name=f"{name}{b}_{s0}")
-        early, late, whole = pieces
         fresh[early] = keep.tile([P, HALF], F32, name="fresh_early")[:]
         fresh[whole] = keep.tile([P, S], F32, name="fresh_whole")[:]
         fresh[late] = gate[whole][:, :HALF]
@@ -161,7 +167,8 @@ def tile_picked_gmem_relu_e_kernel(
             )
 
         old = keep.tile([P, S], F32, name="old", tag=f"x_words{PASSES - 1}", align_bytes=64)
-        nc.vector.tensor_copy(old[:], memory[0][:].indirect(slot_sb[:]))
+        for s0 in range(0, S, HALF):
+            nc.vector.tensor_copy(old[:, s0 : s0 + HALF], memory[0][:].indirect(entries(slot_sb, s0, HALF)))
         for piece in (early, late):
             sigmoid(piece, rest, -1.0)
             sigmoid(piece, gate, 1.0)
@@ -170,6 +177,7 @@ def tile_picked_gmem_relu_e_kernel(
 
         nc.vector.tensor_tensor(kept[early][:], old[:, :HALF], rest[early][:], ALU.mult)
         gated_candidate(early)
+        product(CANDIDATE, late, "candidate_early")
         nc.vector.tensor_tensor(kept[late][:], old[:, HALF:], rest[late][:], ALU.mult)
         put_back(early)
         gated_candidate(whole)

@@ -72,11 +72,12 @@ def tile_picked_gmem_relu_e_kernel(
         nc.sync.dma_start(out=memory[0][:], in_=mem[0:P, :])
         w_words = {}
         for b in range(N // P):
+            if b == 1:
+                nc.sync.dma_start(out=memory[1][:], in_=mem[P : 2 * P, :])
             for i, words in ((GATE, w2_words), (CANDIDATE, w1_words)):
                 w_words[i, b] = keep.tile([P, PASSES, P], U32, name=f"w_words{i}_{b}", align_bytes=64)
                 columns = words[:, :, b * P : (b + 1) * P, :].rearrange("z p n r -> p z (n r)")
                 nc.sync.dma_start(out=w_words[i, b][:].bitcast(I32), in_=columns.bitcast(I32))
-        nc.sync.dma_start(out=memory[1][:], in_=mem[P : 2 * P, :])
 
         def scalar_copy(dst, src):
             nc.scalar.activation(dst, src, ACT.Copy)
@@ -122,68 +123,55 @@ def tile_picked_gmem_relu_e_kernel(
         pieces = ((0, 0, HALF), (0, HALF, HALF), (1, 0, S))
         early, late, whole = pieces
         acc = {}
-
-        def product(i, piece, bank):
+        for piece in pieces:
             b, s0, count = piece
-            acc[i, piece] = psum.tile([P, count], F32, name=f"acc{i}_{b}_{s0}", tag=bank)
-            for z in range(PASSES):
-                nc.tensor.matmul_mx(
-                    out=acc[i, piece][:],
-                    lhsT=w_words[i, b][:, z, :].bitcast(FP8X4),
-                    lhsT_scale=w_scales[SCALE_ROWS * z : P, i * N + b * P : i * N + (b + 1) * P],
-                    rhs=picked_words[z][:, s0 : s0 + count].bitcast(FP8X4),
-                    rhs_scale=picked_bytes[SCALE_ROWS * z : P, s0 : s0 + count],
-                    start=(z == 0),
-                    stop=(z == PASSES - 1),
-                )
-
-        product(GATE, early, "gate_early")
-        product(CANDIDATE, early, "candidate_early")
-        product(GATE, late, "gate_late")
-        product(GATE, whole, "gate_whole")
-        product(CANDIDATE, whole, "candidate_whole")
+            for i in (GATE, CANDIDATE):
+                acc[i, piece] = psum.tile([P, count], F32, name=f"acc{i}_{b}_{s0}")
+                for z in range(PASSES):
+                    nc.tensor.matmul_mx(
+                        out=acc[i, piece][:],
+                        lhsT=w_words[i, b][:, z, :].bitcast(FP8X4),
+                        lhsT_scale=w_scales[SCALE_ROWS * z : P, i * N + b * P : i * N + (b + 1) * P],
+                        rhs=picked_words[z][:, s0 : s0 + count].bitcast(FP8X4),
+                        rhs_scale=picked_bytes[SCALE_ROWS * z : P, s0 : s0 + count],
+                        start=(z == 0),
+                        stop=(z == PASSES - 1),
+                    )
 
         gate, rest, kept, fresh = {}, {}, {}, {}
         for piece in pieces:
             b, s0, count = piece
-            for tiles, name in ((gate, "gate"), (rest, "rest"), (kept, "kept")):
-                tiles[piece] = keep.tile([P, count], F32, name=f"{name}{b}_{s0}")
-        fresh[early] = keep.tile([P, HALF], F32, name="fresh_early")[:]
-        fresh[whole] = keep.tile([P, S], F32, name="fresh_whole")[:]
-        fresh[late] = gate[whole][:, :HALF]
-
-        def sigmoid(piece, tiles, sign):
-            nc.scalar.activation(tiles[piece][:], acc[GATE, piece][:], ACT.Sigmoid, scale=sign)
-
-        def gated_candidate(piece):
-            nc.vector.scalar_tensor_tensor(
-                fresh[piece], acc[CANDIDATE, piece][:], 0.0, gate[piece][:], ALU.max, ALU.mult
-            )
-
-        def put_back(piece):
-            b, s0, count = piece
-            nc.vector.tensor_tensor(
-                memory[b][:].indirect(entries(slot_sb, s0, count)), fresh[piece], kept[piece][:], ALU.add
-            )
-
-        old = keep.tile([P, S], F32, name="old", tag=f"x_words{PASSES - 1}", align_bytes=64)
+            for tiles, name in ((gate, "gate"), (rest, "rest"), (kept, "kept"), (fresh, "fresh")):
+                tiles[piece] = keep.tile([P, count], F32, name=f"{name}{b}_{s0}", tag=f"{name}{b}_{s0}")
+        old = [
+            keep.tile([P, S], F32, name="old0", tag=f"x_words{PASSES - 1}", align_bytes=64),
+            keep.tile([P, S], F32, name="old1"),
+        ]
         for s0 in range(0, S, HALF):
-            nc.vector.tensor_copy(old[:, s0 : s0 + HALF], memory[0][:].indirect(entries(slot_sb, s0, HALF)))
-        for piece in (early, late):
-            sigmoid(piece, rest, -1.0)
-            sigmoid(piece, gate, 1.0)
-        sigmoid(whole, gate, 1.0)
-        sigmoid(whole, rest, -1.0)
+            nc.vector.tensor_copy(old[0][:, s0 : s0 + HALF], memory[0][:].indirect(entries(slot_sb, s0, HALF)))
+        for piece in pieces:
+            nc.scalar.activation(rest[piece][:], acc[GATE, piece][:], ACT.Sigmoid, scale=-1.0)
+            nc.scalar.activation(gate[piece][:], acc[GATE, piece][:], ACT.Sigmoid)
+        candidate = keep.tile([P, S], F32, name="candidate")
+        nc.scalar.activation(candidate[:], acc[CANDIDATE, whole][:], ACT.Relu)
 
-        nc.vector.tensor_tensor(kept[early][:], old[:, :HALF], rest[early][:], ALU.mult)
-        gated_candidate(early)
-        product(CANDIDATE, late, "candidate_early")
-        nc.vector.tensor_tensor(kept[late][:], old[:, HALF:], rest[late][:], ALU.mult)
-        put_back(early)
-        gated_candidate(whole)
-        nc.vector.tensor_tensor(kept[whole][:], memory[1][:].indirect(slot_sb[:]), rest[whole][:], ALU.mult)
-        gated_candidate(late)
-        put_back(whole)
-        nc.sync.dma_start(out=out[P : 2 * P, :], in_=memory[1][:])
-        put_back(late)
+        for piece in (early, late):
+            b, s0, count = piece
+            nc.gpsimd.tensor_tensor(kept[piece][:], old[0][:, s0 : s0 + count], rest[piece][:], ALU.mult)
+            nc.vector.scalar_tensor_tensor(
+                fresh[piece][:], acc[CANDIDATE, piece][:], 0.0, gate[piece][:], ALU.max, ALU.mult
+            )
+        nc.vector.tensor_copy(old[1][:], memory[1][:].indirect(slot_sb[:]))
+        new = {
+            early: keep.tile([P, HALF], F32, name="new_early", tag=f"gate0_{HALF}"),
+            late: keep.tile([P, HALF], F32, name="new_late"),
+        }
+        for piece in (early, late):
+            nc.gpsimd.tensor_tensor(new[piece][:], kept[piece][:], fresh[piece][:], ALU.add)
+        for piece in (early, late):
+            nc.vector.tensor_copy(memory[0][:].indirect(entries(slot_sb, piece[1], HALF)), new[piece][:])
         nc.sync.dma_start(out=out[0:P, :], in_=memory[0][:])
+        nc.gpsimd.tensor_tensor(kept[whole][:], old[1][:], rest[whole][:], ALU.mult)
+        nc.gpsimd.tensor_tensor(fresh[whole][:], candidate[:], gate[whole][:], ALU.mult)
+        nc.vector.tensor_tensor(memory[1][:].indirect(slot_sb[:]), fresh[whole][:], kept[whole][:], ALU.add)
+        nc.sync.dma_start(out=out[P : 2 * P, :], in_=memory[1][:])

@@ -57,27 +57,29 @@ def tile_picked_gmem_relu_e_kernel(
                 c0 = c0 + width
             if z == 0:
                 nc.sync.dma_start(offs_sb[:], offs)
-                nc.sync.dma_start(slot_sb[:], slot)
 
-        w_scales = keep.tile([P, 2 * N], U8, name="w_scales", align_bytes=64)
-        for i, scales, queue in ((GATE, w2_scales, nc.gpsimd), (CANDIDATE, w1_scales, nc.sync)):
-            for q in range(P // QUADRANT):
-                live_rows = slice(QUADRANT * q, QUADRANT * q + SCALE_ROWS * PASSES)
-                queue.dma_start(
-                    out=w_scales[live_rows, i * N : (i + 1) * N].bitcast(I32),
-                    in_=scales[:, SCALE_ROWS * q : SCALE_ROWS * (q + 1), :].bitcast(I32),
-                )
+        w_scales = keep.tile([P, 2, PASSES, N], U8, name="w_scales", align_bytes=64)
+
+        def load_scales(queue, i, scales):
+            rows = scales.rearrange("z (q r) n -> r q z n", r=SCALE_ROWS)
+            for r in range(SCALE_ROWS):
+                queue.dma_start(out=w_scales[r:P:QUADRANT, i].bitcast(I32), in_=rows[r].bitcast(I32))
 
         memory = [keep.tile([P, U], F32, name=f"memory{b}") for b in range(N // P)]
-        nc.sync.dma_start(out=memory[0][:], in_=mem[0:P, :])
         w_words = {}
-        for b in range(N // P):
-            if b == 1:
-                nc.sync.dma_start(out=memory[1][:], in_=mem[P : 2 * P, :])
+
+        def load_block(b):
+            nc.sync.dma_start(out=memory[b][:], in_=mem[b * P : (b + 1) * P, :])
             for i, words in ((GATE, w2_words), (CANDIDATE, w1_words)):
                 w_words[i, b] = keep.tile([P, PASSES, P], U32, name=f"w_words{i}_{b}", align_bytes=64)
                 columns = words[:, :, b * P : (b + 1) * P, :].rearrange("z p n r -> p z (n r)")
                 nc.sync.dma_start(out=w_words[i, b][:].bitcast(I32), in_=columns.bitcast(I32))
+
+        load_scales(nc.gpsimd, GATE, w2_scales)
+        load_block(0)
+        nc.sync.dma_start(slot_sb[:], slot)
+        load_scales(nc.sync, CANDIDATE, w1_scales)
+        load_block(1)
 
         def scalar_copy(dst, src):
             nc.scalar.activation(dst, src, ACT.Copy)
@@ -88,7 +90,7 @@ def tile_picked_gmem_relu_e_kernel(
                 source.rearrange("p j (c i) -> p c j i", i=LINE),
             )
 
-        x_bytes = keep.tile([P, T], U8, name="x_bytes", align_bytes=64)
+        x_bytes = keep.tile([P, T], U8, name="x_bytes", tag="x_bytes", align_bytes=64)
         nc.vector.memset(x_bytes[:].bitcast(I32), 0)
         picked_bytes = keep.tile([P, S], U8, name="picked_bytes", align_bytes=64)
         picked_words = []
@@ -117,8 +119,8 @@ def tile_picked_gmem_relu_e_kernel(
             else:
                 for s0 in range(0, S, HALF):
                     picks = entries(offs_sb, s0, HALF)
-                    nc.vector.tensor_copy(picked[:, s0 : s0 + HALF], x_words[:].indirect(picks))
                     nc.vector.tensor_copy(picked_bytes[:, s0 : s0 + HALF], x_bytes[:].indirect(picks))
+                    nc.vector.tensor_copy(picked[:, s0 : s0 + HALF], x_words[:].indirect(picks))
 
         pieces = ((0, 0, HALF), (0, HALF, HALF), (1, 0, S))
         early, late, whole = pieces
@@ -131,7 +133,7 @@ def tile_picked_gmem_relu_e_kernel(
                     nc.tensor.matmul_mx(
                         out=acc[i, piece][:],
                         lhsT=w_words[i, b][:, z, :].bitcast(FP8X4),
-                        lhsT_scale=w_scales[SCALE_ROWS * z : P, i * N + b * P : i * N + (b + 1) * P],
+                        lhsT_scale=w_scales[:, i, z, b * P : (b + 1) * P],
                         rhs=picked_words[z][:, s0 : s0 + count].bitcast(FP8X4),
                         rhs_scale=picked_bytes[SCALE_ROWS * z : P, s0 : s0 + count],
                         start=(z == 0),
@@ -144,7 +146,7 @@ def tile_picked_gmem_relu_e_kernel(
             for tiles, name in ((gate, "gate"), (rest, "rest"), (kept, "kept"), (fresh, "fresh")):
                 tiles[piece] = keep.tile([P, count], F32, name=f"{name}{b}_{s0}", tag=f"{name}{b}_{s0}")
         old = [
-            keep.tile([P, S], F32, name="old0", tag=f"x_words{PASSES - 1}", align_bytes=64),
+            keep.tile([P, S], F32, name="old0", tag="x_bytes", align_bytes=64),
             keep.tile([P, S], F32, name="old1"),
         ]
         for s0 in range(0, S, HALF):

@@ -144,18 +144,21 @@ def tile_picked_gmem_relu_e_kernel(
         for piece in pieces:
             b, s0, count = piece
             for tiles, name in ((gate, "gate"), (rest, "rest"), (kept, "kept"), (fresh, "fresh")):
-                tiles[piece] = keep.tile([P, count], F32, name=f"{name}{b}_{s0}", tag=f"{name}{b}_{s0}")
+                if (name, piece) != ("kept", whole):
+                    tiles[piece] = keep.tile([P, count], F32, name=f"{name}{b}_{s0}", tag=f"{name}{b}_{s0}")
         old = [
             keep.tile([P, S], F32, name="old0", tag="x_bytes", align_bytes=64),
-            keep.tile([P, S], F32, name="old1"),
+            keep.tile([P, S - P], F32, name="old1"),
         ]
         for s0 in range(0, S, HALF):
             nc.vector.tensor_copy(old[0][:, s0 : s0 + HALF], memory[0][:].indirect(entries(slot_sb, s0, HALF)))
         for piece in pieces:
             nc.scalar.activation(rest[piece][:], acc[GATE, piece][:], ACT.Sigmoid, scale=-1.0)
             nc.scalar.activation(gate[piece][:], acc[GATE, piece][:], ACT.Sigmoid)
-        candidate = keep.tile([P, S], F32, name="candidate")
-        nc.scalar.activation(candidate[:], acc[CANDIDATE, whole][:], ACT.Relu)
+        head = S - P
+        wide = keep.tile([P, head + S], F32, name="wide")
+        kept[whole], candidate = wide[:, :S], wide[:, head:]
+        nc.scalar.activation(candidate, acc[CANDIDATE, whole][:], ACT.Relu)
 
         for piece in (early, late):
             b, s0, count = piece
@@ -163,17 +166,18 @@ def tile_picked_gmem_relu_e_kernel(
             nc.vector.scalar_tensor_tensor(
                 fresh[piece][:], acc[CANDIDATE, piece][:], 0.0, gate[piece][:], ALU.max, ALU.mult
             )
-        nc.vector.tensor_copy(old[1][:], memory[1][:].indirect(slot_sb[:]))
-        new = {
-            early: keep.tile([P, HALF], F32, name="new_early", tag=f"gate0_{HALF}"),
-            late: keep.tile([P, HALF], F32, name="new_late"),
-        }
+        nc.vector.tensor_copy(old[1][:, :head], memory[1][:].indirect(entries(slot_sb, 0, head)))
+        new = {piece: keep.tile([P, HALF], F32, name=f"new{piece[1]}") for piece in (early, late)}
         for piece in (early, late):
             nc.gpsimd.tensor_tensor(new[piece][:], kept[piece][:], fresh[piece][:], ALU.add)
-        for piece in (early, late):
-            nc.vector.tensor_copy(memory[0][:].indirect(entries(slot_sb, piece[1], HALF)), new[piece][:])
+        old_tail = keep.tile([P, P], F32, name="old_tail", tag="fresh0_0")
+        nc.vector.tensor_copy(memory[0][:].indirect(entries(slot_sb, 0, HALF)), new[early][:])
+        nc.vector.tensor_copy(old_tail[:], memory[1][:].indirect(entries(slot_sb, head, P)))
+        nc.vector.tensor_copy(memory[0][:].indirect(entries(slot_sb, HALF, HALF)), new[late][:])
         nc.sync.dma_start(out=out[0:P, :], in_=memory[0][:])
-        nc.gpsimd.tensor_tensor(kept[whole][:], old[1][:], rest[whole][:], ALU.mult)
-        nc.gpsimd.tensor_tensor(fresh[whole][:], candidate[:], gate[whole][:], ALU.mult)
-        nc.vector.tensor_tensor(memory[1][:].indirect(slot_sb[:]), fresh[whole][:], kept[whole][:], ALU.add)
+        nc.gpsimd.tensor_tensor(kept[whole][:, :head], old[1][:, :head], rest[whole][:, :head], ALU.mult)
+        for cols in (slice(0, P), slice(P, S)):
+            nc.gpsimd.tensor_tensor(fresh[whole][:, cols], candidate[:, cols], gate[whole][:, cols], ALU.mult)
+        nc.gpsimd.tensor_tensor(kept[whole][:, head:], old_tail[:], rest[whole][:, head:], ALU.mult)
+        nc.vector.tensor_tensor(memory[1][:].indirect(slot_sb[:]), fresh[whole][:], kept[whole], ALU.add)
         nc.sync.dma_start(out=out[P : 2 * P, :], in_=memory[1][:])

@@ -26,11 +26,6 @@ LANES = 16
 HALF = S // 2
 GATE, CANDIDATE = 0, 1
 
-CHUNKS = (
-    ((256, 256), (64, 192), (160, 96)),
-    ((0, 256), (0, 256), (128, 128), (32, 96), (80, 48)),
-)
-
 
 def tile_picked_gmem_relu_e_kernel(
     tc, xT, mem, w1_words, w1_scales, w2_words, w2_scales, offs, slot, out
@@ -46,81 +41,79 @@ def tile_picked_gmem_relu_e_kernel(
         def entries(list_tile, first, count):
             return list_tile[:, first // LANES : (first + count) // LANES]
 
-        raw = {}
+        nc.sync.dma_start(offs_sb[:], offs)
+        plane = {}
         for z in range(PASSES):
             rows = xT[z * K_PASS : (z + 1) * K_PASS, :].rearrange("(p j) t -> p j t", j=PACK)
-            c0 = 0
-            for n, shares in enumerate(CHUNKS[z]):
-                width = sum(shares)
-                raw[z, n] = keep.tile([P, PACK, width], F32, name=f"raw{z}_{n}")
-                nc.sync.dma_start(out=raw[z, n][:], in_=rows[:, :, c0 : c0 + width])
-                c0 = c0 + width
-            if z == 0:
-                nc.sync.dma_start(offs_sb[:], offs)
+            for j in (0, 2, 1, 3):
+                plane[z, j] = keep.tile([P, T], F32, name=f"plane{z}_{j}")
+                nc.sync.dma_start(out=plane[z, j][:], in_=rows[:, j, :])
 
-        w_scales = keep.tile([P, 2, PASSES, N], U8, name="w_scales", align_bytes=64)
+        w_scales = [keep.tile([P, PASSES, N], U8, name=f"w_scales{i}", align_bytes=64) for i in (GATE, CANDIDATE)]
 
         def load_scales(queue, i, scales):
             rows = scales.rearrange("z (q r) n -> r q z n", r=SCALE_ROWS)
             for r in range(SCALE_ROWS):
-                queue.dma_start(out=w_scales[r:P:QUADRANT, i].bitcast(I32), in_=rows[r].bitcast(I32))
+                queue.dma_start(out=w_scales[i][r:P:QUADRANT].bitcast(I32), in_=rows[r].bitcast(I32))
 
         memory = [keep.tile([P, U], F32, name=f"memory{b}") for b in range(N // P)]
         w_words = {}
 
-        def load_block(b):
+        def load_memory(b):
             nc.sync.dma_start(out=memory[b][:], in_=mem[b * P : (b + 1) * P, :])
-            for i, words in ((GATE, w2_words), (CANDIDATE, w1_words)):
-                w_words[i, b] = keep.tile([P, PASSES, P], U32, name=f"w_words{i}_{b}", align_bytes=64)
-                columns = words[:, :, b * P : (b + 1) * P, :].rearrange("z p n r -> p z (n r)")
-                nc.sync.dma_start(out=w_words[i, b][:].bitcast(I32), in_=columns.bitcast(I32))
+
+        def load_weights(i, b):
+            words = w2_words if i == GATE else w1_words
+            w_words[i, b] = keep.tile([P, PASSES, P], U32, name=f"w_words{i}_{b}", align_bytes=64)
+            columns = words[:, :, b * P : (b + 1) * P, :].rearrange("z p n r -> p z (n r)")
+            nc.sync.dma_start(out=w_words[i, b][:].bitcast(I32), in_=columns.bitcast(I32))
 
         load_scales(nc.gpsimd, GATE, w2_scales)
-        load_block(0)
+        load_scales(nc.scalar, CANDIDATE, w1_scales)
+        load_weights(GATE, 0)
         nc.sync.dma_start(slot_sb[:], slot)
-        load_scales(nc.sync, CANDIDATE, w1_scales)
-        load_block(1)
+        load_memory(0)
+        load_weights(CANDIDATE, 0)
+        load_memory(1)
+        load_weights(GATE, 1)
+        load_weights(CANDIDATE, 1)
 
-        def scalar_copy(dst, src):
+        unread = keep.tile([P, 2], F32, name="unread")
+        nc.vector.memset(unread[:, 0:1], 0.0)
+        nc.scalar.activation(unread[:, 1:2], unread[:, 0:1], ACT.Sigmoid)
+
+        def scalar_round(dst, src):
             nc.scalar.activation(dst, src, ACT.Copy)
 
-        def interleave(copy, grouped, source):
-            copy(
-                grouped.rearrange("p (c i) j -> p c j i", i=LINE),
-                source.rearrange("p j (c i) -> p c j i", i=LINE),
-            )
+        def gpsimd_round(dst, src):
+            nc.gpsimd.tensor_scalar(dst, src, 1.0, 0.0, ALU.mult, ALU.add)
 
-        x_bytes = keep.tile([P, T], U8, name="x_bytes", tag="x_bytes", align_bytes=64)
-        nc.vector.memset(x_bytes[:].bitcast(I32), 0)
-        picked_bytes = keep.tile([P, S], U8, name="picked_bytes", align_bytes=64)
-        picked_words = []
+        rounder = {(0, 0): scalar_round, (0, 1): nc.vector.tensor_copy, (1, 0): scalar_round, (1, 1): gpsimd_round}
+        picked_words, picked_bytes = [], []
         for z in range(PASSES):
-            x_words = keep.tile([P, T], U32, name=f"x_words{z}", tag=f"x_words{z}", align_bytes=64)
-            c0 = 0
-            for n, shares in enumerate(CHUNKS[z]):
-                width = sum(shares)
-                grouped = keep.tile([P, width, PACK], BF16, name=f"grouped{z}_{n}", align_bytes=64)
-                first = 0
-                for share, copy in zip(shares, (nc.vector.tensor_copy, scalar_copy)):
-                    if share > 0:
-                        cols = slice(first, first + share)
-                        interleave(copy, grouped[:, cols, :], raw[z, n][:, :, cols])
-                        first = first + share
+            grouped = keep.tile([P, S, PACK], BF16, name=f"grouped{z}", align_bytes=64)
+            words = keep.tile([P, S], U32, name=f"picked_words{z}", align_bytes=64)
+            scale_bytes = keep.tile([P, S], U8, name=f"picked_bytes{z}", align_bytes=64)
+            picked_words.append(words)
+            picked_bytes.append(scale_bytes)
+            for j in (0, 2, 1, 3):
+                count = HALF if (z == PASSES - 1 and j % 2 == 1) else S
+                if j < 2:
+                    rounded = keep.tile([P, T], BF16, name=f"rounded{z}_{j}", tag=f"rounded{z}_{j}")
+                    rounder[z, j](rounded[:], plane[z, j][:])
+                for s0 in range(0, S, count):
+                    picks = entries(offs_sb, s0, count)
+                    if j < 2:
+                        nc.scalar.activation(grouped[:, s0 : s0 + count, j], rounded[:].indirect(picks), ACT.Copy)
+                    else:
+                        nc.vector.tensor_copy(grouped[:, s0 : s0 + count, j], plane[z, j][:].indirect(picks))
+            count = HALF if z == PASSES - 1 else S
+            for s0 in range(0, S, count):
                 nc.vector.quantize_mx(
-                    out=x_words[:, c0 : c0 + width].bitcast(FP8X4),
-                    scales=x_bytes[SCALE_ROWS * z : P, c0 : c0 + width],
-                    in_=grouped[:].rearrange("p c j -> p (c j)"),
+                    out=words[:, s0 : s0 + count].bitcast(FP8X4),
+                    scales=scale_bytes[:, s0 : s0 + count],
+                    in_=grouped[:, s0 : s0 + count, :].rearrange("p c j -> p (c j)"),
                 )
-                c0 = c0 + width
-            picked = keep.tile([P, S], U32, name=f"picked_words{z}", align_bytes=64)
-            picked_words.append(picked)
-            if z < PASSES - 1:
-                nc.vector.tensor_copy(picked[:], x_words[:].indirect(offs_sb[:]))
-            else:
-                for s0 in range(0, S, HALF):
-                    picks = entries(offs_sb, s0, HALF)
-                    nc.vector.tensor_copy(picked_bytes[:, s0 : s0 + HALF], x_bytes[:].indirect(picks))
-                    nc.vector.tensor_copy(picked[:, s0 : s0 + HALF], x_words[:].indirect(picks))
 
         pieces = ((0, 0, HALF), (0, HALF, HALF), (1, 0, S))
         early, late, whole = pieces
@@ -129,16 +122,25 @@ def tile_picked_gmem_relu_e_kernel(
             b, s0, count = piece
             for i in (GATE, CANDIDATE):
                 acc[i, piece] = psum.tile([P, count], F32, name=f"acc{i}_{b}_{s0}")
-                for z in range(PASSES):
-                    nc.tensor.matmul_mx(
-                        out=acc[i, piece][:],
-                        lhsT=w_words[i, b][:, z, :].bitcast(FP8X4),
-                        lhsT_scale=w_scales[:, i, z, b * P : (b + 1) * P],
-                        rhs=picked_words[z][:, s0 : s0 + count].bitcast(FP8X4),
-                        rhs_scale=picked_bytes[SCALE_ROWS * z : P, s0 : s0 + count],
-                        start=(z == 0),
-                        stop=(z == PASSES - 1),
-                    )
+
+        def product(i, piece, z):
+            b, s0, count = piece
+            nc.tensor.matmul_mx(
+                out=acc[i, piece][:],
+                lhsT=w_words[i, b][:, z, :].bitcast(FP8X4),
+                lhsT_scale=w_scales[i][:, z, b * P : (b + 1) * P],
+                rhs=picked_words[z][:, s0 : s0 + count].bitcast(FP8X4),
+                rhs_scale=picked_bytes[z][:, s0 : s0 + count],
+                start=(z == 0),
+                stop=(z == PASSES - 1),
+            )
+
+        for z in range(PASSES):
+            for piece in (early, late):
+                product(GATE, piece, z)
+        for i, piece in ((CANDIDATE, early), (CANDIDATE, late), (GATE, whole), (CANDIDATE, whole)):
+            for z in range(PASSES):
+                product(i, piece, z)
 
         gate, rest, kept, fresh = {}, {}, {}, {}
         for piece in pieces:
@@ -147,7 +149,7 @@ def tile_picked_gmem_relu_e_kernel(
                 if (name, piece) != ("kept", whole):
                     tiles[piece] = keep.tile([P, count], F32, name=f"{name}{b}_{s0}", tag=f"{name}{b}_{s0}")
         old = [
-            keep.tile([P, S], F32, name="old0", tag="x_bytes", align_bytes=64),
+            keep.tile([P, S], F32, name="old0", tag="rounded1_1"),
             keep.tile([P, S - P], F32, name="old1"),
         ]
         for s0 in range(0, S, HALF):

@@ -47,7 +47,9 @@ def tile_picked_gmem_relu_e_kernel(
             rows = xT[z * K_PASS : (z + 1) * K_PASS, :].rearrange("(p j) t -> p j t", j=PACK)
             for j in (0, 2, 1, 3):
                 plane[z, j] = keep.tile([P, T], F32, name=f"plane{z}_{j}")
-                nc.sync.dma_start(out=plane[z, j][:], in_=rows[:, j, :])
+                width = T // 2 if z == 1 and j < 2 else T
+                for c0 in range(0, T, width):
+                    nc.sync.dma_start(out=plane[z, j][:, c0 : c0 + width], in_=rows[:, j, c0 : c0 + width])
 
         w_scales = [keep.tile([P, PASSES, N], U8, name=f"w_scales{i}", align_bytes=64) for i in (GATE, CANDIDATE)]
 
@@ -62,21 +64,26 @@ def tile_picked_gmem_relu_e_kernel(
         def load_memory(b):
             nc.sync.dma_start(out=memory[b][:], in_=mem[b * P : (b + 1) * P, :])
 
-        def load_weights(i, b):
+        def load_weights(i, passes, blocks):
             words = w2_words if i == GATE else w1_words
-            w_words[i, b] = keep.tile([P, PASSES, P], U32, name=f"w_words{i}_{b}", align_bytes=64)
-            columns = words[:, :, b * P : (b + 1) * P, :].rearrange("z p n r -> p z (n r)")
-            nc.sync.dma_start(out=w_words[i, b][:].bitcast(I32), in_=columns.bitcast(I32))
+            z0, b0 = passes[0], blocks[0]
+            tile = keep.tile([P, len(passes), len(blocks) * P], U32, name=f"w_words{i}_{z0}_{b0}", align_bytes=64)
+            part = words[z0 : z0 + len(passes), :, b0 * P : (b0 + len(blocks)) * P, :]
+            nc.sync.dma_start(out=tile[:].bitcast(I32), in_=part.rearrange("z p n r -> p z (n r)").bitcast(I32))
+            for z in passes:
+                for b in blocks:
+                    w_words[i, z, b] = tile[:, z - z0, (b - b0) * P : (b - b0 + 1) * P]
 
         load_scales(nc.gpsimd, GATE, w2_scales)
         load_scales(nc.scalar, CANDIDATE, w1_scales)
-        load_weights(GATE, 0)
+        load_weights(GATE, (0,), (0, 1))
+        load_weights(GATE, (1,), (0,))
         nc.sync.dma_start(slot_sb[:], slot)
         load_memory(0)
-        load_weights(CANDIDATE, 0)
+        load_weights(CANDIDATE, (0, 1), (0,))
         load_memory(1)
-        load_weights(GATE, 1)
-        load_weights(CANDIDATE, 1)
+        load_weights(GATE, (1,), (1,))
+        load_weights(CANDIDATE, (0, 1), (1,))
 
         unread = keep.tile([P, 2], F32, name="unread")
         nc.vector.memset(unread[:, 0:1], 0.0)
@@ -86,9 +93,11 @@ def tile_picked_gmem_relu_e_kernel(
             nc.scalar.activation(dst, src, ACT.Copy)
 
         def gpsimd_round(dst, src):
-            nc.gpsimd.tensor_scalar(dst, src, 1.0, 0.0, ALU.mult, ALU.add)
+            for c0 in range(0, T, T // 2):
+                cols = slice(c0, c0 + T // 2)
+                nc.gpsimd.tensor_scalar(dst[:, cols], src[:, cols], 1.0, 0.0, ALU.mult, ALU.add)
 
-        rounder = {(0, 0): scalar_round, (0, 1): nc.vector.tensor_copy, (1, 0): scalar_round, (1, 1): gpsimd_round}
+        rounder = {(0, 0): scalar_round, (0, 1): nc.vector.tensor_copy, (1, 0): gpsimd_round, (1, 1): gpsimd_round}
         picked_words, picked_bytes = [], []
         for z in range(PASSES):
             grouped = keep.tile([P, S, PACK], BF16, name=f"grouped{z}", align_bytes=64)
@@ -127,7 +136,7 @@ def tile_picked_gmem_relu_e_kernel(
             b, s0, count = piece
             nc.tensor.matmul_mx(
                 out=acc[i, piece][:],
-                lhsT=w_words[i, b][:, z, :].bitcast(FP8X4),
+                lhsT=w_words[i, z, b].bitcast(FP8X4),
                 lhsT_scale=w_scales[i][:, z, b * P : (b + 1) * P],
                 rhs=picked_words[z][:, s0 : s0 + count].bitcast(FP8X4),
                 rhs_scale=picked_bytes[z][:, s0 : s0 + count],
@@ -135,12 +144,16 @@ def tile_picked_gmem_relu_e_kernel(
                 stop=(z == PASSES - 1),
             )
 
-        for z in range(PASSES):
-            for piece in (early, late):
-                product(GATE, piece, z)
-        for i, piece in ((CANDIDATE, early), (CANDIDATE, late), (GATE, whole), (CANDIDATE, whole)):
+        for piece in pieces:
+            product(GATE, piece, 0)
+        for piece in (early, late):
+            product(GATE, piece, 1)
+        for piece in (early, late):
             for z in range(PASSES):
-                product(i, piece, z)
+                product(CANDIDATE, piece, z)
+        product(GATE, whole, 1)
+        for z in range(PASSES):
+            product(CANDIDATE, whole, z)
 
         gate, rest, kept, fresh = {}, {}, {}, {}
         for piece in pieces:
@@ -149,7 +162,7 @@ def tile_picked_gmem_relu_e_kernel(
                 if (name, piece) != ("kept", whole):
                     tiles[piece] = keep.tile([P, count], F32, name=f"{name}{b}_{s0}", tag=f"{name}{b}_{s0}")
         old = [
-            keep.tile([P, S], F32, name="old0", tag="rounded1_1"),
+            keep.tile([P, S], F32, name="old0"),
             keep.tile([P, S - P], F32, name="old1"),
         ]
         for s0 in range(0, S, HALF):

@@ -46,10 +46,11 @@ def tile_picked_gmem_relu_e_kernel(
         for z in range(PASSES):
             rows = xT[z * K_PASS : (z + 1) * K_PASS, :].rearrange("(p j) t -> p j t", j=PACK)
             for j in (0, 2, 1, 3):
-                plane[z, j] = keep.tile([P, T], F32, name=f"plane{z}_{j}")
-                width = T // 2 if z == 1 and j < 2 else T
+                width = T // 2 if (z, j) == (1, 1) else T
                 for c0 in range(0, T, width):
-                    nc.sync.dma_start(out=plane[z, j][:, c0 : c0 + width], in_=rows[:, j, c0 : c0 + width])
+                    name = f"plane{z}_{j}_{c0}"
+                    plane[z, j, c0] = keep.tile([P, width], F32, name=name, tag=name, align_bytes=64)
+                    nc.sync.dma_start(out=plane[z, j, c0][:], in_=rows[:, j, c0 : c0 + width])
 
         w_scales = [keep.tile([P, PASSES, N], U8, name=f"w_scales{i}", align_bytes=64) for i in (GATE, CANDIDATE)]
 
@@ -67,7 +68,7 @@ def tile_picked_gmem_relu_e_kernel(
         def load_weights(i, passes, blocks):
             words = w2_words if i == GATE else w1_words
             z0, b0 = passes[0], blocks[0]
-            tile = keep.tile([P, len(passes), len(blocks) * P], U32, name=f"w_words{i}_{z0}_{b0}", align_bytes=64)
+            tile = keep.tile([P, len(passes), len(blocks) * P], U32, name=f"w_words{i}_{z0}_{b0}", tag=f"w_words{i}_{z0}_{b0}", align_bytes=64)
             part = words[z0 : z0 + len(passes), :, b0 * P : (b0 + len(blocks)) * P, :]
             nc.sync.dma_start(out=tile[:].bitcast(I32), in_=part.rearrange("z p n r -> p z (n r)").bitcast(I32))
             for z in passes:
@@ -76,123 +77,152 @@ def tile_picked_gmem_relu_e_kernel(
 
         load_scales(nc.gpsimd, GATE, w2_scales)
         load_scales(nc.scalar, CANDIDATE, w1_scales)
-        load_weights(GATE, (0,), (0, 1))
-        load_weights(GATE, (1,), (0,))
+        load_weights(GATE, (0, 1), (0, 1))
         nc.sync.dma_start(slot_sb[:], slot)
         load_memory(0)
-        load_weights(CANDIDATE, (0, 1), (0,))
+        load_weights(CANDIDATE, (0, 1), (0, 1))
         load_memory(1)
-        load_weights(GATE, (1,), (1,))
-        load_weights(CANDIDATE, (0, 1), (1,))
 
         unread = keep.tile([P, 2], F32, name="unread")
         nc.vector.memset(unread[:, 0:1], 0.0)
         nc.scalar.activation(unread[:, 1:2], unread[:, 0:1], ACT.Sigmoid)
 
-        def scalar_round(dst, src):
-            nc.scalar.activation(dst, src, ACT.Copy)
-
-        def gpsimd_round(dst, src):
-            for c0 in range(0, T, T // 2):
-                cols = slice(c0, c0 + T // 2)
-                nc.gpsimd.tensor_scalar(dst[:, cols], src[:, cols], 1.0, 0.0, ALU.mult, ALU.add)
-
-        rounder = {(0, 0): scalar_round, (0, 1): nc.vector.tensor_copy, (1, 0): gpsimd_round, (1, 1): gpsimd_round}
-        picked_words, picked_bytes = [], []
+        spans = {0: ((0, S),), 1: ((0, HALF), (HALF, HALF))}
+        grouped = {
+            (z, s0): keep.tile([P, count, PACK], BF16, name=f"grouped{z}_{s0}", tag=f"grouped{z}_{s0}", align_bytes=64)
+            for z in range(PASSES)
+            for s0, count in spans[z]
+        }
         for z in range(PASSES):
-            grouped = keep.tile([P, S, PACK], BF16, name=f"grouped{z}", align_bytes=64)
-            words = keep.tile([P, S], U32, name=f"picked_words{z}", align_bytes=64)
-            scale_bytes = keep.tile([P, S], U8, name=f"picked_bytes{z}", align_bytes=64)
-            picked_words.append(words)
-            picked_bytes.append(scale_bytes)
             for j in (0, 2, 1, 3):
-                count = HALF if (z == PASSES - 1 and j % 2 == 1) else S
                 if j < 2:
-                    rounded = keep.tile([P, T], BF16, name=f"rounded{z}_{j}", tag=f"rounded{z}_{j}")
-                    rounder[z, j](rounded[:], plane[z, j][:])
-                for s0 in range(0, S, count):
+                    rounded = keep.tile([P, T], BF16, name=f"rounded{z}_{j}")
+                    if (z, j) == (0, 0):
+                        nc.scalar.activation(rounded[:], plane[z, j, 0][:], ACT.Copy)
+                    elif z == 0:
+                        nc.vector.tensor_copy(rounded[:], plane[z, j, 0][:])
+                    else:
+                        width = T // 2 if j == 1 else T
+                        for c0 in range(0, T, width):
+                            nc.gpsimd.tensor_scalar(
+                                rounded[:, c0 : c0 + width], plane[z, j, c0][:], 1.0, 0.0, ALU.mult, ALU.add
+                            )
+                for s0, count in spans[z]:
                     picks = entries(offs_sb, s0, count)
                     if j < 2:
-                        nc.scalar.activation(grouped[:, s0 : s0 + count, j], rounded[:].indirect(picks), ACT.Copy)
+                        nc.scalar.activation(grouped[z, s0][:, :, j], rounded[:].indirect(picks), ACT.Copy)
                     else:
-                        nc.vector.tensor_copy(grouped[:, s0 : s0 + count, j], plane[z, j][:].indirect(picks))
-            count = HALF if z == PASSES - 1 else S
-            for s0 in range(0, S, count):
-                nc.vector.quantize_mx(
-                    out=words[:, s0 : s0 + count].bitcast(FP8X4),
-                    scales=scale_bytes[:, s0 : s0 + count],
-                    in_=grouped[:, s0 : s0 + count, :].rearrange("p c j -> p (c j)"),
-                )
+                        nc.vector.tensor_copy(grouped[z, s0][:, :, j], plane[z, j, 0][:].indirect(picks))
 
-        pieces = ((0, 0, HALF), (0, HALF, HALF), (1, 0, S))
-        early, late, whole = pieces
+        picked_words = [
+            keep.tile([P, S], U32, name="picked_words0", align_bytes=64),
+            keep.tile([P, S], U32, name="picked_words1", align_bytes=64),
+        ]
+        picked_bytes = [keep.tile([P, S], U8, name=f"picked_bytes{z}", align_bytes=64) for z in range(PASSES)]
+
+        def quantise(z, s0, count):
+            nc.vector.quantize_mx(
+                out=picked_words[z][:, s0 : s0 + count].bitcast(FP8X4),
+                scales=picked_bytes[z][:, s0 : s0 + count],
+                in_=grouped[z, s0][:].rearrange("p c j -> p (c j)"),
+            )
+
+        quantise(0, 0, S)
+        for s0 in range(0, S, HALF):
+            quantise(1, s0, HALF)
+
+        pieces = ((0, 0), (1, 0), (0, HALF), (1, HALF))
         acc = {}
-        for piece in pieces:
-            b, s0, count = piece
-            for i in (GATE, CANDIDATE):
-                acc[i, piece] = psum.tile([P, count], F32, name=f"acc{i}_{b}_{s0}")
 
-        def product(i, piece, z):
-            b, s0, count = piece
+        def product(i, piece, z, bank=None):
+            b, s0 = piece
+            if z == 0:
+                name = f"acc{i}_{b}_{s0}"
+                acc[i, piece] = psum.tile([P, HALF], F32, name=name, tag=bank or name)
             nc.tensor.matmul_mx(
                 out=acc[i, piece][:],
                 lhsT=w_words[i, z, b].bitcast(FP8X4),
                 lhsT_scale=w_scales[i][:, z, b * P : (b + 1) * P],
-                rhs=picked_words[z][:, s0 : s0 + count].bitcast(FP8X4),
-                rhs_scale=picked_bytes[z][:, s0 : s0 + count],
+                rhs=picked_words[z][:, s0 : s0 + HALF].bitcast(FP8X4),
+                rhs_scale=picked_bytes[z][:, s0 : s0 + HALF],
                 start=(z == 0),
                 stop=(z == PASSES - 1),
             )
 
-        for piece in pieces:
-            product(GATE, piece, 0)
-        for piece in (early, late):
-            product(GATE, piece, 1)
-        for piece in (early, late):
-            for z in range(PASSES):
-                product(CANDIDATE, piece, z)
-        product(GATE, whole, 1)
-        for z in range(PASSES):
-            product(CANDIDATE, whole, z)
+        def values(name, piece, tag=None):
+            name = f"{name}{piece[0]}_{piece[1]}"
+            return keep.tile([P, HALF], F32, name=name, tag=tag or name)
 
-        gate, rest, kept, fresh = {}, {}, {}, {}
-        for piece in pieces:
-            b, s0, count = piece
-            for tiles, name in ((gate, "gate"), (rest, "rest"), (kept, "kept"), (fresh, "fresh")):
-                if (name, piece) != ("kept", whole):
-                    tiles[piece] = keep.tile([P, count], F32, name=f"{name}{b}_{s0}", tag=f"{name}{b}_{s0}")
-        old = [
-            keep.tile([P, S], F32, name="old0"),
-            keep.tile([P, S - P], F32, name="old1"),
-        ]
-        for s0 in range(0, S, HALF):
-            nc.vector.tensor_copy(old[0][:, s0 : s0 + HALF], memory[0][:].indirect(entries(slot_sb, s0, HALF)))
-        for piece in pieces:
+        gate, rest, candidate, kept, fresh, new = {}, {}, {}, {}, {}, {}
+
+        def sigmoids(piece):
+            rest[piece], gate[piece] = values("rest", piece), values("gate", piece)
             nc.scalar.activation(rest[piece][:], acc[GATE, piece][:], ACT.Sigmoid, scale=-1.0)
             nc.scalar.activation(gate[piece][:], acc[GATE, piece][:], ACT.Sigmoid)
-        head = S - P
-        wide = keep.tile([P, head + S], F32, name="wide")
-        kept[whole], candidate = wide[:, :S], wide[:, head:]
-        nc.scalar.activation(candidate, acc[CANDIDATE, whole][:], ACT.Relu)
 
-        for piece in (early, late):
-            b, s0, count = piece
-            nc.gpsimd.tensor_tensor(kept[piece][:], old[0][:, s0 : s0 + count], rest[piece][:], ALU.mult)
+        def relu(piece):
+            candidate[piece] = values("candidate", piece)
+            nc.scalar.activation(candidate[piece][:], acc[CANDIDATE, piece][:], ACT.Relu)
+
+        for z in range(PASSES):
+            for piece in pieces[:2]:
+                product(GATE, piece, z)
+        for piece in pieces[:2]:
+            sigmoids(piece)
+            for z in range(PASSES):
+                product(CANDIDATE, piece, z)
+        relu(pieces[1])
+        for piece in pieces[2:]:
+            for z in range(PASSES):
+                product(CANDIDATE, piece, z)
+
+        old = [keep.tile([P, S], F32, name=f"old{b}") for b in range(N // P)]
+
+        def keep_old(piece, tag=None):
+            b, s0 = piece
+            kept[piece] = values("kept", piece, tag)
+            nc.gpsimd.tensor_tensor(kept[piece][:], old[b][:, s0 : s0 + HALF], rest[piece][:], ALU.mult)
+
+        def gated_on_vector(piece, tag=None):
+            fresh[piece] = values("fresh", piece, tag)
             nc.vector.scalar_tensor_tensor(
                 fresh[piece][:], acc[CANDIDATE, piece][:], 0.0, gate[piece][:], ALU.max, ALU.mult
             )
-        nc.vector.tensor_copy(old[1][:, :head], memory[1][:].indirect(entries(slot_sb, 0, head)))
-        new = {piece: keep.tile([P, HALF], F32, name=f"new{piece[1]}") for piece in (early, late)}
-        for piece in (early, late):
+
+        def gated_on_gpsimd(piece, tag=None):
+            fresh[piece] = values("fresh", piece, tag)
+            nc.gpsimd.tensor_tensor(fresh[piece][:], candidate[piece][:], gate[piece][:], ALU.mult)
+
+        def add(piece):
+            new[piece] = values("new", piece)
             nc.gpsimd.tensor_tensor(new[piece][:], kept[piece][:], fresh[piece][:], ALU.add)
-        old_tail = keep.tile([P, P], F32, name="old_tail", tag="fresh0_0")
-        nc.vector.tensor_copy(memory[0][:].indirect(entries(slot_sb, 0, HALF)), new[early][:])
-        nc.vector.tensor_copy(old_tail[:], memory[1][:].indirect(entries(slot_sb, head, P)))
-        nc.vector.tensor_copy(memory[0][:].indirect(entries(slot_sb, HALF, HALF)), new[late][:])
+
+        def window(piece):
+            return memory[piece[0]][:].indirect(entries(slot_sb, piece[1], HALF))
+
+        first, second, third, fourth = pieces
+        for s0 in range(0, S, HALF):
+            nc.vector.tensor_copy(old[0][:, s0 : s0 + HALF], window((0, s0)))
+        keep_old(first)
+        gated_on_vector(first)
+        for piece in pieces[2:]:
+            for z in range(PASSES):
+                product(GATE, piece, z, bank=f"acc{CANDIDATE}_{piece[0]}_0")
+            sigmoids(piece)
+        relu(fourth)
+        nc.vector.tensor_copy(old[1][:], memory[1][:].indirect(slot_sb[:]))
+        add(first)
+        gated_on_gpsimd(second)
+        keep_old(second)
+        add(second)
+        nc.vector.tensor_copy(window(first), new[first][:])
+        gated_on_vector(third, tag="fresh0_0")
+        keep_old(third, tag="kept1_0")
+        add(third)
+        nc.vector.tensor_copy(window(second), new[second][:])
+        nc.vector.tensor_copy(window(third), new[third][:])
         nc.sync.dma_start(out=out[0:P, :], in_=memory[0][:])
-        nc.gpsimd.tensor_tensor(kept[whole][:, :head], old[1][:, :head], rest[whole][:, :head], ALU.mult)
-        for cols in (slice(0, P), slice(P, S)):
-            nc.gpsimd.tensor_tensor(fresh[whole][:, cols], candidate[:, cols], gate[whole][:, cols], ALU.mult)
-        nc.gpsimd.tensor_tensor(kept[whole][:, head:], old_tail[:], rest[whole][:, head:], ALU.mult)
-        nc.vector.tensor_tensor(memory[1][:].indirect(slot_sb[:]), fresh[whole][:], kept[whole], ALU.add)
+        gated_on_gpsimd(fourth, tag="fresh0_0")
+        keep_old(fourth, tag="kept1_0")
+        nc.vector.tensor_tensor(window(fourth), fresh[fourth][:], kept[fourth][:], ALU.add)
         nc.sync.dma_start(out=out[P : 2 * P, :], in_=memory[1][:])

@@ -41,7 +41,6 @@ def tile_picked_gmem_relu_e_kernel(
         def entries(list_tile, first, count):
             return list_tile[:, first // LANES : (first + count) // LANES]
 
-        nc.sync.dma_start(offs_sb[:], offs)
         plane = {}
         for z in range(PASSES):
             rows = xT[z * K_PASS : (z + 1) * K_PASS, :].rearrange("(p j) t -> p j t", j=PACK)
@@ -51,6 +50,8 @@ def tile_picked_gmem_relu_e_kernel(
                     name = f"plane{z}_{j}_{c0}"
                     plane[z, j, c0] = keep.tile([P, width], F32, name=name, tag=name, align_bytes=64)
                     nc.sync.dma_start(out=plane[z, j, c0][:], in_=rows[:, j, c0 : c0 + width])
+                if (z, j) == (0, 0):
+                    nc.sync.dma_start(offs_sb[:], offs)
 
         w_scales = [keep.tile([P, PASSES, N], U8, name=f"w_scales{i}", align_bytes=64) for i in (GATE, CANDIDATE)]
 
@@ -97,10 +98,8 @@ def tile_picked_gmem_relu_e_kernel(
             for j in (0, 2, 1, 3):
                 if j < 2:
                     rounded = keep.tile([P, T], BF16, name=f"rounded{z}_{j}")
-                    if (z, j) == (0, 0):
+                    if z == 0:
                         nc.scalar.activation(rounded[:], plane[z, j, 0][:], ACT.Copy)
-                    elif z == 0:
-                        nc.vector.tensor_copy(rounded[:], plane[z, j, 0][:])
                     else:
                         width = T // 2 if j == 1 else T
                         for c0 in range(0, T, width):
@@ -155,33 +154,36 @@ def tile_picked_gmem_relu_e_kernel(
 
         gate, rest, candidate, kept, fresh, new = {}, {}, {}, {}, {}, {}
 
-        def sigmoids(piece):
+        def sigmoids(piece, gate_first=False):
             rest[piece], gate[piece] = values("rest", piece), values("gate", piece)
-            nc.scalar.activation(rest[piece][:], acc[GATE, piece][:], ACT.Sigmoid, scale=-1.0)
-            nc.scalar.activation(gate[piece][:], acc[GATE, piece][:], ACT.Sigmoid)
+            for sign in (1.0, -1.0) if gate_first else (-1.0, 1.0):
+                made = gate if sign > 0 else rest
+                nc.scalar.activation(made[piece][:], acc[GATE, piece][:], ACT.Sigmoid, scale=sign)
 
-        def relu(piece):
+        def relu(piece, cols=slice(0, HALF)):
             candidate[piece] = values("candidate", piece)
-            nc.scalar.activation(candidate[piece][:], acc[CANDIDATE, piece][:], ACT.Relu)
+            nc.scalar.activation(candidate[piece][:, cols], acc[CANDIDATE, piece][:, cols], ACT.Relu)
 
         for z in range(PASSES):
             for piece in pieces[:2]:
                 product(GATE, piece, z)
         for piece in pieces[:2]:
-            sigmoids(piece)
+            sigmoids(piece, gate_first=False)
             for z in range(PASSES):
                 product(CANDIDATE, piece, z)
-        relu(pieces[1])
         for piece in pieces[2:]:
             for z in range(PASSES):
                 product(CANDIDATE, piece, z)
 
-        old = [keep.tile([P, S], F32, name=f"old{b}") for b in range(N // P)]
+        old = {}
 
         def keep_old(piece, tag=None):
-            b, s0 = piece
             kept[piece] = values("kept", piece, tag)
-            nc.gpsimd.tensor_tensor(kept[piece][:], old[b][:, s0 : s0 + HALF], rest[piece][:], ALU.mult)
+            nc.gpsimd.tensor_tensor(kept[piece][:], old[piece][:], rest[piece][:], ALU.mult)
+
+        def fetch_old(piece):
+            old[piece] = values("old", piece)
+            nc.vector.tensor_copy(old[piece][:], window(piece))
 
         def gated_on_vector(piece, tag=None):
             fresh[piece] = values("fresh", piece, tag)
@@ -200,29 +202,39 @@ def tile_picked_gmem_relu_e_kernel(
         def window(piece):
             return memory[piece[0]][:].indirect(entries(slot_sb, piece[1], HALF))
 
-        first, second, third, fourth = pieces
-        for s0 in range(0, S, HALF):
-            nc.vector.tensor_copy(old[0][:, s0 : s0 + HALF], window((0, s0)))
-        keep_old(first)
-        gated_on_vector(first)
-        for piece in pieces[2:]:
+        def late_gate(piece):
             for z in range(PASSES):
                 product(GATE, piece, z, bank=f"acc{CANDIDATE}_{piece[0]}_0")
             sigmoids(piece)
+
+        first, second, third, fourth = pieces
+        fetch_old(first)
+        fetch_old(third)
+        keep_old(first)
+        gated_on_vector(first)
+        head, tail = slice(0, P), slice(P, HALF)
+        relu(third, tail)
         relu(fourth)
-        nc.vector.tensor_copy(old[1][:], memory[1][:].indirect(slot_sb[:]))
+        late_gate(third)
+        fetch_old(second)
+        fetch_old(fourth)
         add(first)
-        gated_on_gpsimd(second)
+        gated_on_vector(second, tag="fresh0_0")
+        late_gate(fourth)
         keep_old(second)
         add(second)
+        keep_old(third, tag="rest1_0")
+        fresh[third] = values("fresh", third, "old1_0")
+        nc.gpsimd.tensor_tensor(fresh[third][:, tail], candidate[third][:, tail], gate[third][:, tail], ALU.mult)
         nc.vector.tensor_copy(window(first), new[first][:])
-        gated_on_vector(third, tag="fresh0_0")
-        keep_old(third, tag="kept1_0")
+        nc.vector.scalar_tensor_tensor(
+            fresh[third][:, head], acc[CANDIDATE, third][:, head], 0.0, gate[third][:, head], ALU.max, ALU.mult
+        )
         add(third)
-        nc.vector.tensor_copy(window(second), new[second][:])
-        nc.vector.tensor_copy(window(third), new[third][:])
+        keep_old(fourth, tag="rest1_0")
+        gated_on_gpsimd(fourth, tag="old1_0")
+        for piece in pieces[1:3]:
+            nc.vector.tensor_copy(window(piece), new[piece][:])
         nc.sync.dma_start(out=out[0:P, :], in_=memory[0][:])
-        gated_on_gpsimd(fourth, tag="fresh0_0")
-        keep_old(fourth, tag="kept1_0")
         nc.vector.tensor_tensor(window(fourth), fresh[fourth][:], kept[fourth][:], ALU.add)
         nc.sync.dma_start(out=out[P : 2 * P, :], in_=memory[1][:])

@@ -98,10 +98,12 @@ def tile_picked_gmem_relu_e_kernel(
             for j in (0, 2, 1, 3):
                 if j < 2:
                     rounded = keep.tile([P, T], BF16, name=f"rounded{z}_{j}")
-                    if z == 0:
+                    if j == 0:
                         nc.scalar.activation(rounded[:], plane[z, j, 0][:], ACT.Copy)
+                    elif z == 0:
+                        nc.vector.tensor_copy(rounded[:], plane[z, j, 0][:])
                     else:
-                        width = T // 2 if j == 1 else T
+                        width = T // 2
                         for c0 in range(0, T, width):
                             nc.gpsimd.tensor_scalar(
                                 rounded[:, c0 : c0 + width], plane[z, j, c0][:], 1.0, 0.0, ALU.mult, ALU.add
@@ -160,9 +162,9 @@ def tile_picked_gmem_relu_e_kernel(
                 made = gate if sign > 0 else rest
                 nc.scalar.activation(made[piece][:], acc[GATE, piece][:], ACT.Sigmoid, scale=sign)
 
-        def relu(piece, cols=slice(0, HALF)):
+        def relu(piece):
             candidate[piece] = values("candidate", piece)
-            nc.scalar.activation(candidate[piece][:, cols], acc[CANDIDATE, piece][:, cols], ACT.Relu)
+            nc.scalar.activation(candidate[piece][:], acc[CANDIDATE, piece][:], ACT.Relu)
 
         for z in range(PASSES):
             for piece in pieces[:2]:
@@ -212,9 +214,8 @@ def tile_picked_gmem_relu_e_kernel(
         fetch_old(third)
         keep_old(first)
         gated_on_vector(first)
-        head, tail = slice(0, P), slice(P, HALF)
-        relu(third, tail)
-        relu(fourth)
+        for piece in pieces[2:]:
+            relu(piece)
         late_gate(third)
         fetch_old(second)
         fetch_old(fourth)
@@ -224,16 +225,11 @@ def tile_picked_gmem_relu_e_kernel(
         keep_old(second)
         add(second)
         keep_old(third, tag="rest1_0")
-        fresh[third] = values("fresh", third, "old1_0")
-        nc.gpsimd.tensor_tensor(fresh[third][:, tail], candidate[third][:, tail], gate[third][:, tail], ALU.mult)
-        nc.vector.tensor_copy(window(first), new[first][:])
-        nc.vector.scalar_tensor_tensor(
-            fresh[third][:, head], acc[CANDIDATE, third][:, head], 0.0, gate[third][:, head], ALU.max, ALU.mult
-        )
+        gated_on_gpsimd(third, tag="old1_0")
         add(third)
         keep_old(fourth, tag="rest1_0")
         gated_on_gpsimd(fourth, tag="old1_0")
-        for piece in pieces[1:3]:
+        for piece in pieces[:3]:
             nc.vector.tensor_copy(window(piece), new[piece][:])
         nc.sync.dma_start(out=out[0:P, :], in_=memory[0][:])
         nc.vector.tensor_tensor(window(fourth), fresh[fourth][:], kept[fourth][:], ALU.add)

@@ -21,9 +21,10 @@ K_PASS = P * PACK
 PASSES = K // K_PASS
 QUADRANT = 32
 SCALE_ROWS = 4
-LINE = 4
 LANES = 16
+LINE = 8
 HALF = S // 2
+EARLY, LATE = 0, HALF
 GATE, CANDIDATE = 0, 1
 
 
@@ -38,20 +39,20 @@ def tile_picked_gmem_relu_e_kernel(
         offs_sb = keep.tile([P, S // LANES], U16, name="offs_sb")
         slot_sb = keep.tile([P, S // LANES], U16, name="slot_sb")
 
-        def entries(list_tile, first, count):
-            return list_tile[:, first // LANES : (first + count) // LANES]
+        def entries(list_tile, first):
+            return list_tile[:, first // LANES : (first + HALF) // LANES]
 
-        plane = {}
-        for z in range(PASSES):
+        plane, w_words = {}, {}
+
+        def load_plane(z, j):
             rows = xT[z * K_PASS : (z + 1) * K_PASS, :].rearrange("(p j) t -> p j t", j=PACK)
-            for j in (0, 2, 1, 3):
-                width = T // 2 if (z, j) == (1, 1) else T
-                for c0 in range(0, T, width):
-                    name = f"plane{z}_{j}_{c0}"
-                    plane[z, j, c0] = keep.tile([P, width], F32, name=name, tag=name, align_bytes=64)
-                    nc.sync.dma_start(out=plane[z, j, c0][:], in_=rows[:, j, c0 : c0 + width])
-                if (z, j) == (0, 0):
-                    nc.sync.dma_start(offs_sb[:], offs)
+            plane[z, j] = keep.tile([P, T], F32, name=f"plane{z}_{j}", align_bytes=64)
+            nc.sync.dma_start(out=plane[z, j][:], in_=rows[:, j, :])
+
+        def load_weights(i, z):
+            words = w2_words if i == GATE else w1_words
+            w_words[i, z] = keep.tile([P, N], U32, name=f"w_words{i}_{z}", align_bytes=64)
+            nc.sync.dma_start(out=w_words[i, z][:].bitcast(I32), in_=words[z].rearrange("p n r -> p (n r)").bitcast(I32))
 
         w_scales = [keep.tile([P, PASSES, N], U8, name=f"w_scales{i}", align_bytes=64) for i in (GATE, CANDIDATE)]
 
@@ -61,176 +62,111 @@ def tile_picked_gmem_relu_e_kernel(
                 queue.dma_start(out=w_scales[i][r:P:QUADRANT].bitcast(I32), in_=rows[r].bitcast(I32))
 
         memory = [keep.tile([P, U], F32, name=f"memory{b}") for b in range(N // P)]
-        w_words = {}
 
         def load_memory(b):
             nc.sync.dma_start(out=memory[b][:], in_=mem[b * P : (b + 1) * P, :])
 
-        def load_weights(i, passes, blocks):
-            words = w2_words if i == GATE else w1_words
-            z0, b0 = passes[0], blocks[0]
-            tile = keep.tile([P, len(passes), len(blocks) * P], U32, name=f"w_words{i}_{z0}_{b0}", tag=f"w_words{i}_{z0}_{b0}", align_bytes=64)
-            part = words[z0 : z0 + len(passes), :, b0 * P : (b0 + len(blocks)) * P, :]
-            nc.sync.dma_start(out=tile[:].bitcast(I32), in_=part.rearrange("z p n r -> p z (n r)").bitcast(I32))
-            for z in passes:
-                for b in blocks:
-                    w_words[i, z, b] = tile[:, z - z0, (b - b0) * P : (b - b0 + 1) * P]
-
-        load_scales(nc.gpsimd, GATE, w2_scales)
-        load_scales(nc.scalar, CANDIDATE, w1_scales)
-        load_weights(GATE, (0, 1), (0, 1))
+        load_plane(0, 0)
+        nc.sync.dma_start(offs_sb[:], offs)
+        for j in range(1, PACK):
+            load_plane(0, j)
+        for j in range(PACK - 1):
+            load_plane(1, j)
+        load_weights(GATE, 0)
+        load_weights(CANDIDATE, 0)
+        load_plane(1, PACK - 1)
         nc.sync.dma_start(slot_sb[:], slot)
         load_memory(0)
-        load_weights(CANDIDATE, (0, 1), (0, 1))
+        load_weights(GATE, 1)
+        load_weights(CANDIDATE, 1)
         load_memory(1)
+        load_scales(nc.gpsimd, GATE, w2_scales)
+        load_scales(nc.scalar, CANDIDATE, w1_scales)
 
         unread = keep.tile([P, 2], F32, name="unread")
         nc.vector.memset(unread[:, 0:1], 0.0)
         nc.scalar.activation(unread[:, 1:2], unread[:, 0:1], ACT.Sigmoid)
 
-        spans = {0: ((0, S),), 1: ((0, HALF), (HALF, HALF))}
-        grouped = {
-            (z, s0): keep.tile([P, count, PACK], BF16, name=f"grouped{z}_{s0}", tag=f"grouped{z}_{s0}", align_bytes=64)
-            for z in range(PASSES)
-            for s0, count in spans[z]
-        }
-        for z in range(PASSES):
-            for j in (0, 2, 1, 3):
-                if j < 2:
-                    rounded = keep.tile([P, T], BF16, name=f"rounded{z}_{j}")
-                    if j == 0:
-                        nc.scalar.activation(rounded[:], plane[z, j, 0][:], ACT.Copy)
-                    elif z == 0:
-                        nc.vector.tensor_copy(rounded[:], plane[z, j, 0][:])
-                    else:
-                        width = T // 2
-                        for c0 in range(0, T, width):
-                            nc.gpsimd.tensor_scalar(
-                                rounded[:, c0 : c0 + width], plane[z, j, c0][:], 1.0, 0.0, ALU.mult, ALU.add
-                            )
-                for s0, count in spans[z]:
-                    picks = entries(offs_sb, s0, count)
-                    if j < 2:
-                        nc.scalar.activation(grouped[z, s0][:, :, j], rounded[:].indirect(picks), ACT.Copy)
-                    else:
-                        nc.vector.tensor_copy(grouped[z, s0][:, :, j], plane[z, j, 0][:].indirect(picks))
+        words, scale_bytes, grouped = {}, {}, {}
 
-        picked_words = [
-            keep.tile([P, S], U32, name="picked_words0", align_bytes=64),
-            keep.tile([P, S], U32, name="picked_words1", align_bytes=64),
-        ]
-        picked_bytes = [keep.tile([P, S], U8, name=f"picked_bytes{z}", align_bytes=64) for z in range(PASSES)]
+        def gather_pass(z):
+            for s0 in (EARLY, LATE):
+                grouped[z, s0] = keep.tile([P, HALF, PACK], BF16, name=f"grouped{z}_{s0}", align_bytes=64)
+            rows = keep.tile([P, PACK, HALF], BF16, name=f"rows{z}", align_bytes=64)
+            for j in range(PACK):
+                nc.vector.tensor_copy(grouped[z, EARLY][:, :, j], plane[z, j][:].indirect(entries(offs_sb, EARLY)))
+                nc.scalar.activation(rows[:, j, :], plane[z, j][:].indirect(entries(offs_sb, LATE)), ACT.Copy)
+            nc.scalar.copy(
+                grouped[z, LATE][:].rearrange("p (c i) j -> p c j i", i=LINE),
+                rows[:].rearrange("p j (c i) -> p c j i", i=LINE),
+            )
 
-        def quantise(z, s0, count):
+        def quantise(z, s0):
+            words[z, s0] = keep.tile([P, HALF], U32, name=f"words{z}_{s0}", align_bytes=64)
+            scale_bytes[z, s0] = keep.tile([P, HALF], U8, name=f"bytes{z}_{s0}", align_bytes=64)
             nc.vector.quantize_mx(
-                out=picked_words[z][:, s0 : s0 + count].bitcast(FP8X4),
-                scales=picked_bytes[z][:, s0 : s0 + count],
+                out=words[z, s0][:].bitcast(FP8X4),
+                scales=scale_bytes[z, s0][:],
                 in_=grouped[z, s0][:].rearrange("p c j -> p (c j)"),
             )
 
-        quantise(0, 0, S)
-        for s0 in range(0, S, HALF):
-            quantise(1, s0, HALF)
-
-        pieces = ((0, 0), (1, 0), (0, HALF), (1, HALF))
         acc = {}
 
-        def product(i, piece, z, bank=None):
-            b, s0 = piece
+        def product(i, b, s0, z):
             if z == 0:
-                name = f"acc{i}_{b}_{s0}"
-                acc[i, piece] = psum.tile([P, HALF], F32, name=name, tag=bank or name)
+                acc[i, b, s0] = psum.tile([P, HALF], F32, name=f"acc{i}_{b}_{s0}")
             nc.tensor.matmul_mx(
-                out=acc[i, piece][:],
-                lhsT=w_words[i, z, b].bitcast(FP8X4),
+                out=acc[i, b, s0][:],
+                lhsT=w_words[i, z][:, b * P : (b + 1) * P].bitcast(FP8X4),
                 lhsT_scale=w_scales[i][:, z, b * P : (b + 1) * P],
-                rhs=picked_words[z][:, s0 : s0 + HALF].bitcast(FP8X4),
-                rhs_scale=picked_bytes[z][:, s0 : s0 + HALF],
+                rhs=words[z, s0][:].bitcast(FP8X4),
+                rhs_scale=scale_bytes[z, s0][:],
                 start=(z == 0),
                 stop=(z == PASSES - 1),
             )
 
-        def values(name, piece, tag=None):
-            name = f"{name}{piece[0]}_{piece[1]}"
-            return keep.tile([P, HALF], F32, name=name, tag=tag or name)
+        def products(z, s0):
+            for b in range(N // P):
+                for i in (GATE, CANDIDATE):
+                    product(i, b, s0, z)
 
-        gate, rest, candidate, kept, fresh, new = {}, {}, {}, {}, {}, {}
+        def values(name, b, s0):
+            return keep.tile([P, HALF], F32, name=f"{name}{b}_{s0}")
 
-        def sigmoids(piece, gate_first=False):
-            rest[piece], gate[piece] = values("rest", piece), values("gate", piece)
-            for sign in (1.0, -1.0) if gate_first else (-1.0, 1.0):
-                made = gate if sign > 0 else rest
-                nc.scalar.activation(made[piece][:], acc[GATE, piece][:], ACT.Sigmoid, scale=sign)
+        def window(b, s0):
+            return memory[b][:].indirect(entries(slot_sb, s0))
 
-        def relu(piece):
-            candidate[piece] = values("candidate", piece)
-            nc.scalar.activation(candidate[piece][:], acc[CANDIDATE, piece][:], ACT.Relu)
+        gather_pass(0)
+        quantise(0, EARLY)
+        quantise(0, LATE)
+        gather_pass(1)
+        products(0, EARLY)
+        products(0, LATE)
+        quantise(1, EARLY)
+        old = {s0: values("old", 0, s0) for s0 in (EARLY, LATE)}
+        nc.vector.tensor_copy(old[EARLY][:], window(0, EARLY))
+        quantise(1, LATE)
+        products(1, EARLY)
+        products(1, LATE)
 
-        for z in range(PASSES):
-            for piece in pieces[:2]:
-                product(GATE, piece, z)
-        for piece in pieces[:2]:
-            sigmoids(piece, gate_first=False)
-            for z in range(PASSES):
-                product(CANDIDATE, piece, z)
-        for piece in pieces[2:]:
-            for z in range(PASSES):
-                product(CANDIDATE, piece, z)
-
-        old = {}
-
-        def keep_old(piece, tag=None):
-            kept[piece] = values("kept", piece, tag)
-            nc.gpsimd.tensor_tensor(kept[piece][:], old[piece][:], rest[piece][:], ALU.mult)
-
-        def fetch_old(piece):
-            old[piece] = values("old", piece)
-            nc.vector.tensor_copy(old[piece][:], window(piece))
-
-        def gated_on_vector(piece, tag=None):
-            fresh[piece] = values("fresh", piece, tag)
-            nc.vector.scalar_tensor_tensor(
-                fresh[piece][:], acc[CANDIDATE, piece][:], 0.0, gate[piece][:], ALU.max, ALU.mult
-            )
-
-        def gated_on_gpsimd(piece, tag=None):
-            fresh[piece] = values("fresh", piece, tag)
-            nc.gpsimd.tensor_tensor(fresh[piece][:], candidate[piece][:], gate[piece][:], ALU.mult)
-
-        def add(piece):
-            new[piece] = values("new", piece)
-            nc.gpsimd.tensor_tensor(new[piece][:], kept[piece][:], fresh[piece][:], ALU.add)
-
-        def window(piece):
-            return memory[piece[0]][:].indirect(entries(slot_sb, piece[1], HALF))
-
-        def late_gate(piece):
-            for z in range(PASSES):
-                product(GATE, piece, z, bank=f"acc{CANDIDATE}_{piece[0]}_0")
-            sigmoids(piece)
-
-        first, second, third, fourth = pieces
-        fetch_old(first)
-        fetch_old(third)
-        keep_old(first)
-        gated_on_vector(first)
-        for piece in pieces[2:]:
-            relu(piece)
-        late_gate(third)
-        fetch_old(second)
-        fetch_old(fourth)
-        add(first)
-        gated_on_vector(second, tag="fresh0_0")
-        late_gate(fourth)
-        keep_old(second)
-        add(second)
-        keep_old(third, tag="rest1_0")
-        gated_on_gpsimd(third, tag="old1_0")
-        add(third)
-        keep_old(fourth, tag="rest1_0")
-        gated_on_gpsimd(fourth, tag="old1_0")
-        for piece in pieces[:3]:
-            nc.vector.tensor_copy(window(piece), new[piece][:])
+        new0, kept, fresh = {}, {}, {}
+        for s0 in (EARLY, LATE):
+            gate0, gate1, rest1 = values("gate", 0, s0), values("gate", 1, s0), values("rest", 1, s0)
+            nc.scalar.activation(gate0[:], acc[GATE, 0, s0][:], ACT.Sigmoid)
+            nc.scalar.activation(gate1[:], acc[GATE, 1, s0][:], ACT.Sigmoid)
+            nc.scalar.activation(rest1[:], acc[GATE, 1, s0][:], ACT.Sigmoid, scale=-1.0)
+            if s0 == EARLY:
+                nc.scalar.activation(old[LATE][:], window(0, LATE), ACT.Copy)
+            step, move = values("step", 0, s0), values("move", 0, s0)
+            new0[s0], kept[s0], fresh[s0] = values("new", 0, s0), values("kept", 1, s0), values("fresh", 1, s0)
+            nc.vector.scalar_tensor_tensor(step[:], acc[CANDIDATE, 0, s0][:], 0.0, old[s0][:], ALU.max, ALU.subtract)
+            nc.vector.scalar_tensor_tensor(fresh[s0][:], acc[CANDIDATE, 1, s0][:], 0.0, gate1[:], ALU.max, ALU.mult)
+            nc.vector.tensor_tensor(move[:], step[:], gate0[:], ALU.mult)
+            nc.vector.tensor_tensor(kept[s0][:], window(1, s0), rest1[:], ALU.mult)
+            nc.vector.tensor_tensor(new0[s0][:], move[:], old[s0][:], ALU.add)
+        for s0 in (EARLY, LATE):
+            nc.scalar.activation(window(0, s0), new0[s0][:], ACT.Copy)
         nc.sync.dma_start(out=out[0:P, :], in_=memory[0][:])
-        nc.vector.tensor_tensor(window(fourth), fresh[fourth][:], kept[fourth][:], ALU.add)
+        for s0 in (EARLY, LATE):
+            nc.vector.tensor_tensor(window(1, s0), fresh[s0][:], kept[s0][:], ALU.add)
         nc.sync.dma_start(out=out[P : 2 * P, :], in_=memory[1][:])

@@ -70,12 +70,12 @@ def tile_picked_gmem_relu_e_kernel(
         nc.sync.dma_start(offs_sb[:], offs)
         for j in range(1, PACK):
             load_plane(0, j)
+        nc.sync.dma_start(slot_sb[:], slot)
         for j in range(PACK - 1):
             load_plane(1, j)
         load_weights(GATE, 0)
         load_weights(CANDIDATE, 0)
         load_plane(1, PACK - 1)
-        nc.sync.dma_start(slot_sb[:], slot)
         load_memory(0)
         load_weights(GATE, 1)
         load_weights(CANDIDATE, 1)
@@ -89,17 +89,25 @@ def tile_picked_gmem_relu_e_kernel(
 
         words, scale_bytes, grouped = {}, {}, {}
 
+        def weave(engine_copy, z, rows, j0, c0, count):
+            engine_copy(
+                grouped[z, LATE][:, c0 : c0 + count, j0 : j0 + 2].rearrange("p (c i) j -> p c j i", i=LINE),
+                rows[:, :, c0 : c0 + count].rearrange("p j (c i) -> p c j i", i=LINE),
+            )
+
         def gather_pass(z):
             for s0 in (EARLY, LATE):
                 grouped[z, s0] = keep.tile([P, HALF, PACK], BF16, name=f"grouped{z}_{s0}", align_bytes=64)
-            rows = keep.tile([P, PACK, HALF], BF16, name=f"rows{z}", align_bytes=64)
-            for j in range(PACK):
-                nc.vector.tensor_copy(grouped[z, EARLY][:, :, j], plane[z, j][:].indirect(entries(offs_sb, EARLY)))
-                nc.scalar.activation(rows[:, j, :], plane[z, j][:].indirect(entries(offs_sb, LATE)), ACT.Copy)
-            nc.scalar.copy(
-                grouped[z, LATE][:].rearrange("p (c i) j -> p c j i", i=LINE),
-                rows[:].rearrange("p j (c i) -> p c j i", i=LINE),
-            )
+            for j0 in (0, 2):
+                rows = keep.tile([P, 2, HALF], BF16, name=f"rows{z}_{j0}", align_bytes=64)
+                for j in (j0, j0 + 1):
+                    nc.vector.tensor_copy(grouped[z, EARLY][:, :, j], plane[z, j][:].indirect(entries(offs_sb, EARLY)))
+                    nc.scalar.activation(rows[:, j - j0, :], plane[z, j][:].indirect(entries(offs_sb, LATE)), ACT.Copy)
+                if (z, j0) == (PASSES - 1, 2):
+                    weave(nc.vector.tensor_copy, z, rows, j0, 0, HALF // 2)
+                    weave(nc.scalar.copy, z, rows, j0, HALF // 2, HALF // 2)
+                else:
+                    weave(nc.scalar.copy, z, rows, j0, 0, HALF)
 
         def quantise(z, s0):
             words[z, s0] = keep.tile([P, HALF], U32, name=f"words{z}_{s0}", align_bytes=64)
@@ -127,7 +135,7 @@ def tile_picked_gmem_relu_e_kernel(
 
         def products(z, s0):
             for b in range(N // P):
-                for i in (GATE, CANDIDATE):
+                for i in (CANDIDATE, GATE):
                     product(i, b, s0, z)
 
         def values(name, b, s0):
@@ -143,30 +151,45 @@ def tile_picked_gmem_relu_e_kernel(
         products(0, EARLY)
         products(0, LATE)
         quantise(1, EARLY)
-        old = {s0: values("old", 0, s0) for s0 in (EARLY, LATE)}
-        nc.vector.tensor_copy(old[EARLY][:], window(0, EARLY))
         quantise(1, LATE)
         products(1, EARLY)
         products(1, LATE)
 
-        new0, kept, fresh = {}, {}, {}
-        for s0 in (EARLY, LATE):
-            gate0, gate1, rest1 = values("gate", 0, s0), values("gate", 1, s0), values("rest", 1, s0)
-            nc.scalar.activation(gate0[:], acc[GATE, 0, s0][:], ACT.Sigmoid)
-            nc.scalar.activation(gate1[:], acc[GATE, 1, s0][:], ACT.Sigmoid)
-            nc.scalar.activation(rest1[:], acc[GATE, 1, s0][:], ACT.Sigmoid, scale=-1.0)
-            if s0 == EARLY:
-                nc.scalar.activation(old[LATE][:], window(0, LATE), ACT.Copy)
-            step, move = values("step", 0, s0), values("move", 0, s0)
-            new0[s0], kept[s0], fresh[s0] = values("new", 0, s0), values("kept", 1, s0), values("fresh", 1, s0)
-            nc.vector.scalar_tensor_tensor(step[:], acc[CANDIDATE, 0, s0][:], 0.0, old[s0][:], ALU.max, ALU.subtract)
-            nc.vector.scalar_tensor_tensor(fresh[s0][:], acc[CANDIDATE, 1, s0][:], 0.0, gate1[:], ALU.max, ALU.mult)
-            nc.vector.tensor_tensor(move[:], step[:], gate0[:], ALU.mult)
-            nc.vector.tensor_tensor(kept[s0][:], window(1, s0), rest1[:], ALU.mult)
-            nc.vector.tensor_tensor(new0[s0][:], move[:], old[s0][:], ALU.add)
-        for s0 in (EARLY, LATE):
-            nc.scalar.activation(window(0, s0), new0[s0][:], ACT.Copy)
+        halves = (EARLY, LATE)
+        old, gate, step, move, new = {}, {}, {}, {}, {}
+
+        def fetch_old(b):
+            for s0 in halves:
+                old[b, s0] = values("old", b, s0)
+                nc.scalar.activation(old[b, s0][:], window(b, s0), ACT.Copy)
+
+        def gates(b):
+            for s0 in halves:
+                gate[b, s0] = values("gate", b, s0)
+                nc.scalar.activation(gate[b, s0][:], acc[GATE, b, s0][:], ACT.Sigmoid)
+
+        def moves(b):
+            for s0 in halves:
+                step[b, s0] = values("step", b, s0)
+                nc.vector.scalar_tensor_tensor(
+                    step[b, s0][:], acc[CANDIDATE, b, s0][:], 0.0, old[b, s0][:], ALU.max, ALU.subtract
+                )
+            for s0 in halves:
+                move[b, s0] = values("move", b, s0)
+                nc.vector.tensor_tensor(move[b, s0][:], step[b, s0][:], gate[b, s0][:], ALU.mult)
+
+        fetch_old(0)
+        gates(0)
+        fetch_old(1)
+        gates(1)
+        moves(0)
+        for s0 in halves:
+            new[s0] = values("new", 0, s0)
+            nc.vector.tensor_tensor(new[s0][:], move[0, s0][:], old[0, s0][:], ALU.add)
+        moves(1)
+        for s0 in halves:
+            nc.scalar.activation(window(0, s0), new[s0][:], ACT.Copy)
         nc.sync.dma_start(out=out[0:P, :], in_=memory[0][:])
-        for s0 in (EARLY, LATE):
-            nc.vector.tensor_tensor(window(1, s0), fresh[s0][:], kept[s0][:], ALU.add)
+        for s0 in halves:
+            nc.vector.tensor_tensor(window(1, s0), move[1, s0][:], old[1, s0][:], ALU.add)
         nc.sync.dma_start(out=out[P : 2 * P, :], in_=memory[1][:])

@@ -73,8 +73,8 @@ def tile_picked_gmem_relu_e_kernel(
         nc.sync.dma_start(slot_sb[:], slot)
         for j in range(PACK - 1):
             load_plane(1, j)
-        load_weights(GATE, 0)
         load_weights(CANDIDATE, 0)
+        load_weights(GATE, 0)
         load_plane(1, PACK - 1)
         load_memory(0)
         load_weights(GATE, 1)
@@ -110,7 +110,9 @@ def tile_picked_gmem_relu_e_kernel(
                     weave(nc.scalar.copy, z, rows, j0, 0, HALF)
 
         def quantise(z, s0):
-            words[z, s0] = keep.tile([P, HALF], U32, name=f"words{z}_{s0}", align_bytes=64)
+            name = f"words{z}_{s0}"
+            tag = f"plane{z}_{PACK - 1}" if (z, s0) == (PASSES - 1, EARLY) else name
+            words[z, s0] = keep.tile([P, HALF], U32, name=name, tag=tag, align_bytes=64)
             scale_bytes[z, s0] = keep.tile([P, HALF], U8, name=f"bytes{z}_{s0}", align_bytes=64)
             nc.vector.quantize_mx(
                 out=words[z, s0][:].bitcast(FP8X4),
@@ -161,7 +163,10 @@ def tile_picked_gmem_relu_e_kernel(
         def fetch_old(b):
             for s0 in halves:
                 old[b, s0] = values("old", b, s0)
-                nc.scalar.activation(old[b, s0][:], window(b, s0), ACT.Copy)
+                if (b, s0) == (0, LATE):
+                    nc.vector.tensor_copy(old[b, s0][:], window(b, s0))
+                else:
+                    nc.scalar.activation(old[b, s0][:], window(b, s0), ACT.Copy)
 
         def gates(b):
             for s0 in halves:

@@ -39,8 +39,8 @@ def tile_picked_gmem_relu_e_kernel(
         offs_sb = keep.tile([P, S // LANES], U16, name="offs_sb")
         slot_sb = keep.tile([P, S // LANES], U16, name="slot_sb")
 
-        def entries(list_tile, first):
-            return list_tile[:, first // LANES : (first + HALF) // LANES]
+        def entries(list_tile, first, count=HALF):
+            return list_tile[:, first // LANES : (first + count) // LANES]
 
         plane, w_words = {}, {}
 
@@ -123,16 +123,20 @@ def tile_picked_gmem_relu_e_kernel(
         acc = {}
 
         def product(i, b, s0, z):
-            if z == 0:
-                acc[i, b, s0] = psum.tile([P, HALF], F32, name=f"acc{i}_{b}_{s0}")
+            shared = (i, s0) in ((CANDIDATE, EARLY), (GATE, LATE))
+            if z == 0 and (i, s0) == (CANDIDATE, EARLY):
+                bank = psum.tile([P, S], F32, name=f"bank{b}")
+                acc[CANDIDATE, b, EARLY], acc[GATE, b, LATE] = bank[:, 0:HALF], bank[:, HALF:S]
+            elif z == 0 and not shared:
+                acc[i, b, s0] = psum.tile([P, HALF], F32, name=f"acc{i}_{b}_{s0}")[:]
             nc.tensor.matmul_mx(
-                out=acc[i, b, s0][:],
+                out=acc[i, b, s0],
                 lhsT=w_words[i, z][:, b * P : (b + 1) * P].bitcast(FP8X4),
                 lhsT_scale=w_scales[i][:, z, b * P : (b + 1) * P],
                 rhs=words[z, s0][:].bitcast(FP8X4),
                 rhs_scale=scale_bytes[z, s0][:],
-                start=(z == 0),
-                stop=(z == PASSES - 1),
+                start=(z == 0 and (i, s0) != (GATE, LATE)),
+                stop=(z == PASSES - 1 and (i, s0) != (CANDIDATE, EARLY)),
             )
 
         def products(z, s0):
@@ -143,8 +147,8 @@ def tile_picked_gmem_relu_e_kernel(
         def values(name, b, s0):
             return keep.tile([P, HALF], F32, name=f"{name}{b}_{s0}")
 
-        def window(b, s0):
-            return memory[b][:].indirect(entries(slot_sb, s0))
+        def window(b, s0, count=HALF):
+            return memory[b][:].indirect(entries(slot_sb, s0, count))
 
         gather_pass(0)
         quantise(0, EARLY)
@@ -154,8 +158,9 @@ def tile_picked_gmem_relu_e_kernel(
         products(0, LATE)
         quantise(1, EARLY)
         quantise(1, LATE)
-        products(1, EARLY)
-        products(1, LATE)
+        for b in range(N // P):
+            for i, s0 in ((GATE, EARLY), (CANDIDATE, EARLY), (GATE, LATE), (CANDIDATE, LATE)):
+                product(i, b, s0, 1)
 
         halves = (EARLY, LATE)
         old, gate, step, move, new = {}, {}, {}, {}, {}
@@ -165,32 +170,46 @@ def tile_picked_gmem_relu_e_kernel(
                 old[b, s0] = values("old", b, s0)
                 if (b, s0) == (0, LATE):
                     nc.vector.tensor_copy(old[b, s0][:], window(b, s0))
+                elif (b, s0) == (1, LATE):
+                    cut = HALF // 2
+                    nc.scalar.activation(old[b, s0][:, :cut], window(b, s0, cut), ACT.Copy)
                 else:
                     nc.scalar.activation(old[b, s0][:], window(b, s0), ACT.Copy)
 
-        def gates(b):
-            for s0 in halves:
-                gate[b, s0] = values("gate", b, s0)
-                nc.scalar.activation(gate[b, s0][:], acc[GATE, b, s0][:], ACT.Sigmoid)
+        def make_gate(b, s0):
+            gate[b, s0] = values("gate", b, s0)
+            nc.scalar.activation(gate[b, s0][:], acc[GATE, b, s0], ACT.Sigmoid)
+
+        def make_step(b, s0):
+            step[b, s0] = values("step", b, s0)
+            nc.vector.scalar_tensor_tensor(
+                step[b, s0][:], acc[CANDIDATE, b, s0], 0.0, old[b, s0][:], ALU.max, ALU.subtract
+            )
 
         def moves(b):
-            for s0 in halves:
-                step[b, s0] = values("step", b, s0)
-                nc.vector.scalar_tensor_tensor(
-                    step[b, s0][:], acc[CANDIDATE, b, s0][:], 0.0, old[b, s0][:], ALU.max, ALU.subtract
-                )
             for s0 in halves:
                 move[b, s0] = values("move", b, s0)
                 nc.vector.tensor_tensor(move[b, s0][:], step[b, s0][:], gate[b, s0][:], ALU.mult)
 
         fetch_old(0)
-        gates(0)
+        for s0 in halves:
+            if s0 == EARLY:
+                make_gate(0, s0)
+            make_step(0, s0)
+            if s0 == EARLY:
+                make_gate(0, LATE)
         fetch_old(1)
-        gates(1)
+        for s0 in halves:
+            make_gate(1, s0)
         moves(0)
         for s0 in halves:
             new[s0] = values("new", 0, s0)
-            nc.vector.tensor_tensor(new[s0][:], move[0, s0][:], old[0, s0][:], ALU.add)
+            engine = nc.vector if s0 == EARLY else nc.gpsimd
+            engine.tensor_tensor(new[s0][:], move[0, s0][:], old[0, s0][:], ALU.add)
+        cut = HALF // 2
+        nc.vector.tensor_copy(old[1, LATE][:, cut:], window(1, LATE + cut, cut))
+        for s0 in halves:
+            make_step(1, s0)
         moves(1)
         for s0 in halves:
             nc.scalar.activation(window(0, s0), new[s0][:], ACT.Copy)

@@ -169,10 +169,9 @@ def tile_picked_gmem_relu_e_kernel(
             for s0 in halves:
                 old[b, s0] = values("old", b, s0)
                 if (b, s0) == (0, LATE):
-                    nc.vector.tensor_copy(old[b, s0][:], window(b, s0))
-                elif (b, s0) == (1, LATE):
                     cut = HALF // 2
                     nc.scalar.activation(old[b, s0][:, :cut], window(b, s0, cut), ACT.Copy)
+                    nc.vector.tensor_copy(old[b, s0][:, cut:], window(b, s0 + cut, cut))
                 else:
                     nc.scalar.activation(old[b, s0][:], window(b, s0), ACT.Copy)
 
@@ -206,8 +205,6 @@ def tile_picked_gmem_relu_e_kernel(
             new[s0] = values("new", 0, s0)
             engine = nc.vector if s0 == EARLY else nc.gpsimd
             engine.tensor_tensor(new[s0][:], move[0, s0][:], old[0, s0][:], ALU.add)
-        cut = HALF // 2
-        nc.vector.tensor_copy(old[1, LATE][:, cut:], window(1, LATE + cut, cut))
         for s0 in halves:
             make_step(1, s0)
         moves(1)

@@ -17,15 +17,20 @@ ACT = mybir.ActivationFunctionType
 
 P = 128
 PACK = 4
+PAIR = 2
 K_PASS = P * PACK
 PASSES = K // K_PASS
+LAST_PASS = PASSES - 1
+BLOCKS = N // P
 QUADRANT = 32
 SCALE_ROWS = 4
 LANES = 16
 LINE = 8
 HALF = S // 2
 EARLY, LATE = 0, HALF
+HALVES = (EARLY, LATE)
 GATE, CANDIDATE = 0, 1
+SHARE = HALF // 2
 
 
 def tile_picked_gmem_relu_e_kernel(
@@ -50,9 +55,9 @@ def tile_picked_gmem_relu_e_kernel(
             nc.sync.dma_start(out=plane[z, j][:], in_=rows[:, j, :])
 
         def load_weights(i, z):
-            words = w2_words if i == GATE else w1_words
+            packed = w2_words if i == GATE else w1_words
             w_words[i, z] = keep.tile([P, N], U32, name=f"w_words{i}_{z}", align_bytes=64)
-            nc.sync.dma_start(out=w_words[i, z][:].bitcast(I32), in_=words[z].rearrange("p n r -> p (n r)").bitcast(I32))
+            nc.sync.dma_start(out=w_words[i, z][:].bitcast(I32), in_=packed[z].rearrange("p n r -> p (n r)").bitcast(I32))
 
         w_scales = [keep.tile([P, PASSES, N], U8, name=f"w_scales{i}", align_bytes=64) for i in (GATE, CANDIDATE)]
 
@@ -61,7 +66,7 @@ def tile_picked_gmem_relu_e_kernel(
             for r in range(SCALE_ROWS):
                 queue.dma_start(out=w_scales[i][r:P:QUADRANT].bitcast(I32), in_=rows[r].bitcast(I32))
 
-        memory = [keep.tile([P, U], F32, name=f"memory{b}") for b in range(N // P)]
+        memory = [keep.tile([P, U], F32, name=f"memory{b}") for b in range(BLOCKS)]
 
         def load_memory(b):
             nc.sync.dma_start(out=memory[b][:], in_=mem[b * P : (b + 1) * P, :])
@@ -72,13 +77,13 @@ def tile_picked_gmem_relu_e_kernel(
             load_plane(0, j)
         nc.sync.dma_start(slot_sb[:], slot)
         for j in range(PACK - 1):
-            load_plane(1, j)
+            load_plane(LAST_PASS, j)
         load_weights(CANDIDATE, 0)
+        load_plane(LAST_PASS, PACK - 1)
         load_weights(GATE, 0)
-        load_plane(1, PACK - 1)
         load_memory(0)
-        load_weights(GATE, 1)
-        load_weights(CANDIDATE, 1)
+        load_weights(GATE, LAST_PASS)
+        load_weights(CANDIDATE, LAST_PASS)
         load_memory(1)
         load_scales(nc.gpsimd, GATE, w2_scales)
         load_scales(nc.scalar, CANDIDATE, w1_scales)
@@ -91,27 +96,27 @@ def tile_picked_gmem_relu_e_kernel(
 
         def weave(engine_copy, z, rows, j0, c0, count):
             engine_copy(
-                grouped[z, LATE][:, c0 : c0 + count, j0 : j0 + 2].rearrange("p (c i) j -> p c j i", i=LINE),
+                grouped[z, LATE][:, c0 : c0 + count, j0 : j0 + PAIR].rearrange("p (c i) j -> p c j i", i=LINE),
                 rows[:, :, c0 : c0 + count].rearrange("p j (c i) -> p c j i", i=LINE),
             )
 
         def gather_pass(z):
-            for s0 in (EARLY, LATE):
+            for s0 in HALVES:
                 grouped[z, s0] = keep.tile([P, HALF, PACK], BF16, name=f"grouped{z}_{s0}", align_bytes=64)
-            for j0 in (0, 2):
-                rows = keep.tile([P, 2, HALF], BF16, name=f"rows{z}_{j0}", align_bytes=64)
-                for j in (j0, j0 + 1):
+            for j0 in range(0, PACK, PAIR):
+                rows = keep.tile([P, PAIR, HALF], BF16, name=f"rows{z}_{j0}", align_bytes=64)
+                for j in range(j0, j0 + PAIR):
                     nc.vector.tensor_copy(grouped[z, EARLY][:, :, j], plane[z, j][:].indirect(entries(offs_sb, EARLY)))
                     nc.scalar.activation(rows[:, j - j0, :], plane[z, j][:].indirect(entries(offs_sb, LATE)), ACT.Copy)
-                if (z, j0) == (PASSES - 1, 2):
-                    weave(nc.vector.tensor_copy, z, rows, j0, 0, HALF // 2)
-                    weave(nc.scalar.copy, z, rows, j0, HALF // 2, HALF // 2)
+                if (z, j0) == (LAST_PASS, PACK - PAIR):
+                    weave(nc.vector.tensor_copy, z, rows, j0, 0, SHARE)
+                    weave(nc.scalar.copy, z, rows, j0, SHARE, HALF - SHARE)
                 else:
                     weave(nc.scalar.copy, z, rows, j0, 0, HALF)
 
         def quantise(z, s0):
             name = f"words{z}_{s0}"
-            tag = f"plane{z}_{PACK - 1}" if (z, s0) == (PASSES - 1, EARLY) else name
+            tag = f"plane{z}_{PACK - 1}" if (z, s0) == (LAST_PASS, EARLY) else name
             words[z, s0] = keep.tile([P, HALF], U32, name=name, tag=tag, align_bytes=64)
             scale_bytes[z, s0] = keep.tile([P, HALF], U8, name=f"bytes{z}_{s0}", align_bytes=64)
             nc.vector.quantize_mx(
@@ -123,11 +128,7 @@ def tile_picked_gmem_relu_e_kernel(
         acc = {}
 
         def product(i, b, s0, z):
-            shared = (i, s0) in ((CANDIDATE, EARLY), (GATE, LATE))
-            if z == 0 and (i, s0) == (CANDIDATE, EARLY):
-                bank = psum.tile([P, S], F32, name=f"bank{b}")
-                acc[CANDIDATE, b, EARLY], acc[GATE, b, LATE] = bank[:, 0:HALF], bank[:, HALF:S]
-            elif z == 0 and not shared:
+            if z == 0:
                 acc[i, b, s0] = psum.tile([P, HALF], F32, name=f"acc{i}_{b}_{s0}")[:]
             nc.tensor.matmul_mx(
                 out=acc[i, b, s0],
@@ -135,43 +136,40 @@ def tile_picked_gmem_relu_e_kernel(
                 lhsT_scale=w_scales[i][:, z, b * P : (b + 1) * P],
                 rhs=words[z, s0][:].bitcast(FP8X4),
                 rhs_scale=scale_bytes[z, s0][:],
-                start=(z == 0 and (i, s0) != (GATE, LATE)),
-                stop=(z == PASSES - 1 and (i, s0) != (CANDIDATE, EARLY)),
+                start=(z == 0),
+                stop=(z == LAST_PASS),
             )
 
-        def products(z, s0):
-            for b in range(N // P):
+        gather_pass(0)
+        for s0 in HALVES:
+            quantise(0, s0)
+        gather_pass(LAST_PASS)
+        for s0 in HALVES:
+            for b in range(BLOCKS):
                 for i in (CANDIDATE, GATE):
-                    product(i, b, s0, z)
+                    product(i, b, s0, 0)
+        for s0 in HALVES:
+            quantise(LAST_PASS, s0)
+        for s0 in HALVES:
+            for b in range(BLOCKS):
+                product(GATE, b, s0, LAST_PASS)
+        for b in range(BLOCKS):
+            for s0 in HALVES:
+                product(CANDIDATE, b, s0, LAST_PASS)
+
+        old, gate, step, move, new = {}, {}, {}, {}, {}
 
         def values(name, b, s0):
             return keep.tile([P, HALF], F32, name=f"{name}{b}_{s0}")
 
-        def window(b, s0, count=HALF):
-            return memory[b][:].indirect(entries(slot_sb, s0, count))
-
-        gather_pass(0)
-        quantise(0, EARLY)
-        quantise(0, LATE)
-        gather_pass(1)
-        products(0, EARLY)
-        products(0, LATE)
-        quantise(1, EARLY)
-        quantise(1, LATE)
-        for b in range(N // P):
-            for i, s0 in ((GATE, EARLY), (CANDIDATE, EARLY), (GATE, LATE), (CANDIDATE, LATE)):
-                product(i, b, s0, 1)
-
-        halves = (EARLY, LATE)
-        old, gate, step, move, new = {}, {}, {}, {}, {}
+        def window(b, first, count=HALF):
+            return memory[b][:].indirect(entries(slot_sb, first, count))
 
         def fetch_old(b):
-            for s0 in halves:
+            for s0 in HALVES:
                 old[b, s0] = values("old", b, s0)
                 if (b, s0) == (0, LATE):
-                    cut = HALF // 2
-                    nc.scalar.activation(old[b, s0][:, :cut], window(b, s0, cut), ACT.Copy)
-                    nc.vector.tensor_copy(old[b, s0][:, cut:], window(b, s0 + cut, cut))
+                    nc.vector.tensor_copy(old[b, s0][:], window(b, s0))
                 else:
                     nc.scalar.activation(old[b, s0][:], window(b, s0), ACT.Copy)
 
@@ -185,32 +183,30 @@ def tile_picked_gmem_relu_e_kernel(
                 step[b, s0][:], acc[CANDIDATE, b, s0], 0.0, old[b, s0][:], ALU.max, ALU.subtract
             )
 
-        def moves(b):
-            for s0 in halves:
+        def make_moves(b):
+            for s0 in HALVES:
                 move[b, s0] = values("move", b, s0)
                 nc.vector.tensor_tensor(move[b, s0][:], step[b, s0][:], gate[b, s0][:], ALU.mult)
 
         fetch_old(0)
-        for s0 in halves:
-            if s0 == EARLY:
-                make_gate(0, s0)
-            make_step(0, s0)
-            if s0 == EARLY:
-                make_gate(0, LATE)
+        make_gate(0, EARLY)
+        make_step(0, EARLY)
+        make_gate(0, LATE)
+        make_step(0, LATE)
         fetch_old(1)
-        for s0 in halves:
+        for s0 in HALVES:
             make_gate(1, s0)
-        moves(0)
-        for s0 in halves:
+        make_moves(0)
+        for s0, engine in ((EARLY, nc.vector), (LATE, nc.gpsimd)):
             new[s0] = values("new", 0, s0)
-            engine = nc.vector if s0 == EARLY else nc.gpsimd
             engine.tensor_tensor(new[s0][:], move[0, s0][:], old[0, s0][:], ALU.add)
-        for s0 in halves:
+        for s0 in HALVES:
             make_step(1, s0)
-        moves(1)
-        for s0 in halves:
+        make_moves(1)
+
+        for s0 in HALVES:
             nc.scalar.activation(window(0, s0), new[s0][:], ACT.Copy)
         nc.sync.dma_start(out=out[0:P, :], in_=memory[0][:])
-        for s0 in halves:
+        for s0 in HALVES:
             nc.vector.tensor_tensor(window(1, s0), move[1, s0][:], old[1, s0][:], ALU.add)
         nc.sync.dma_start(out=out[P : 2 * P, :], in_=memory[1][:])

from contextlib import ExitStack

import concourse.mybir as mybir

K, T, S, N, U = 1024, 1024, 512, 256, 1024
FLOPS = 2 * 2 * K * N * S

F32 = mybir.dt.float32
BF16 = mybir.dt.bfloat16
I32 = mybir.dt.int32
U32 = mybir.dt.uint32
U16 = mybir.dt.uint16
U8 = mybir.dt.uint8
FP8X4 = mybir.dt.float8_e4m3fn_x4
ALU = mybir.AluOpType
ACT = mybir.ActivationFunctionType

P = 128
PACK = 4
PAIR = 2
K_PASS = P * PACK
PASSES = K // K_PASS
LAST_PASS = PASSES - 1
BLOCKS = N // P
QUADRANT = 32
SCALE_ROWS = 4
LANES = 16
LINE = 8
HALF = S // 2
EARLY, LATE = 0, HALF
HALVES = (EARLY, LATE)
GATE, CANDIDATE = 0, 1
SHARE = HALF // 2


def tile_picked_gmem_relu_e_kernel(
    tc, xT, mem, w1_words, w1_scales, w2_words, w2_scales, offs, slot, out
):
    nc = tc.nc
    with ExitStack() as ctx:
        keep = ctx.enter_context(tc.tile_pool(name="keep", bufs=1))
        psum = ctx.enter_context(tc.psum_pool(name="psum", bufs=1))

        offs_sb = keep.tile([P, S // LANES], U16, name="offs_sb")
        slot_sb = keep.tile([P, S // LANES], U16, name="slot_sb")

        def entries(list_tile, first, count=HALF):
            return list_tile[:, first // LANES : (first + count) // LANES]

        plane, w_words = {}, {}

        def load_plane(z, j):
            rows = xT[z * K_PASS : (z + 1) * K_PASS, :].rearrange("(p j) t -> p j t", j=PACK)
            plane[z, j] = keep.tile([P, T], F32, name=f"plane{z}_{j}", align_bytes=64)
            nc.sync.dma_start(out=plane[z, j][:], in_=rows[:, j, :])

        def load_weights(i, z):
            packed = w2_words if i == GATE else w1_words
            w_words[i, z] = keep.tile([P, N], U32, name=f"w_words{i}_{z}", align_bytes=64)
            nc.sync.dma_start(out=w_words[i, z][:].bitcast(I32), in_=packed[z].rearrange("p n r -> p (n r)").bitcast(I32))

        w_scales = [keep.tile([P, PASSES, N], U8, name=f"w_scales{i}", align_bytes=64) for i in (GATE, CANDIDATE)]

        def load_scales(queue, i, scales):
            rows = scales.rearrange("z (q r) n -> r q z n", r=SCALE_ROWS)
            for r in range(SCALE_ROWS):
                queue.dma_start(out=w_scales[i][r:P:QUADRANT].bitcast(I32), in_=rows[r].bitcast(I32))

        memory = [keep.tile([P, U], F32, name=f"memory{b}") for b in range(BLOCKS)]

        def load_memory(b):
            nc.sync.dma_start(out=memory[b][:], in_=mem[b * P : (b + 1) * P, :])

        load_plane(0, 0)
        nc.sync.dma_start(offs_sb[:], offs)
        for j in range(1, PACK):
            load_plane(0, j)
        nc.sync.dma_start(slot_sb[:], slot)
        for j in range(PACK - 1):
            load_plane(LAST_PASS, j)
        load_weights(CANDIDATE, 0)
        load_plane(LAST_PASS, PACK - 1)
        load_weights(GATE, 0)
        load_memory(0)
        load_weights(GATE, LAST_PASS)
        load_weights(CANDIDATE, LAST_PASS)
        load_memory(1)
        load_scales(nc.gpsimd, GATE, w2_scales)
        load_scales(nc.scalar, CANDIDATE, w1_scales)

        unread = keep.tile([P, 2], F32, name="unread")
        nc.vector.memset(unread[:, 0:1], 0.0)
        nc.scalar.activation(unread[:, 1:2], unread[:, 0:1], ACT.Sigmoid)

        words, scale_bytes, grouped = {}, {}, {}

        def weave(engine_copy, z, rows, j0, c0, count):
            engine_copy(
                grouped[z, LATE][:, c0 : c0 + count, j0 : j0 + PAIR].rearrange("p (c i) j -> p c j i", i=LINE),
                rows[:, :, c0 : c0 + count].rearrange("p j (c i) -> p c j i", i=LINE),
            )

        def gather_pass(z):
            for s0 in HALVES:
                grouped[z, s0] = keep.tile([P, HALF, PACK], BF16, name=f"grouped{z}_{s0}", align_bytes=64)
            for j0 in range(0, PACK, PAIR):
                rows = keep.tile([P, PAIR, HALF], BF16, name=f"rows{z}_{j0}", align_bytes=64)
                for j in range(j0, j0 + PAIR):
                    nc.vector.tensor_copy(grouped[z, EARLY][:, :, j], plane[z, j][:].indirect(entries(offs_sb, EARLY)))
                    nc.scalar.activation(rows[:, j - j0, :], plane[z, j][:].indirect(entries(offs_sb, LATE)), ACT.Copy)
                if (z, j0) == (LAST_PASS, PACK - PAIR):
                    weave(nc.vector.tensor_copy, z, rows, j0, 0, SHARE)
                    weave(nc.scalar.copy, z, rows, j0, SHARE, HALF - SHARE)
                else:
                    weave(nc.scalar.copy, z, rows, j0, 0, HALF)

        def quantise(z, s0):
            name = f"words{z}_{s0}"
            tag = f"plane{z}_{PACK - 1}" if (z, s0) == (LAST_PASS, EARLY) else name
            words[z, s0] = keep.tile([P, HALF], U32, name=name, tag=tag, align_bytes=64)
            scale_bytes[z, s0] = keep.tile([P, HALF], U8, name=f"bytes{z}_{s0}", align_bytes=64)
            nc.vector.quantize_mx(
                out=words[z, s0][:].bitcast(FP8X4),
                scales=scale_bytes[z, s0][:],
                in_=grouped[z, s0][:].rearrange("p c j -> p (c j)"),
            )

        acc = {}

        def product(i, b, s0, z):
            if z == 0:
                acc[i, b, s0] = psum.tile([P, HALF], F32, name=f"acc{i}_{b}_{s0}")[:]
            nc.tensor.matmul_mx(
                out=acc[i, b, s0],
                lhsT=w_words[i, z][:, b * P : (b + 1) * P].bitcast(FP8X4),
                lhsT_scale=w_scales[i][:, z, b * P : (b + 1) * P],
                rhs=words[z, s0][:].bitcast(FP8X4),
                rhs_scale=scale_bytes[z, s0][:],
                start=(z == 0),
                stop=(z == LAST_PASS),
            )

        gather_pass(0)
        for s0 in HALVES:
            quantise(0, s0)
        gather_pass(LAST_PASS)
        for s0 in HALVES:
            for b in range(BLOCKS):
                for i in (CANDIDATE, GATE):
                    product(i, b, s0, 0)
        for s0 in HALVES:
            quantise(LAST_PASS, s0)
        for s0 in HALVES:
            for b in range(BLOCKS):
                product(GATE, b, s0, LAST_PASS)
        for b in range(BLOCKS):
            for s0 in HALVES:
                product(CANDIDATE, b, s0, LAST_PASS)

        old, gate, step, move, new = {}, {}, {}, {}, {}

        def values(name, b, s0):
            return keep.tile([P, HALF], F32, name=f"{name}{b}_{s0}")

        def window(b, first, count=HALF):
            return memory[b][:].indirect(entries(slot_sb, first, count))

        def fetch_old(b):
            for s0 in HALVES:
                old[b, s0] = values("old", b, s0)
                if (b, s0) == (0, LATE):
                    nc.vector.tensor_copy(old[b, s0][:], window(b, s0))
                else:
                    nc.scalar.activation(old[b, s0][:], window(b, s0), ACT.Copy)

        def make_gate(b, s0):
            gate[b, s0] = values("gate", b, s0)
            nc.scalar.activation(gate[b, s0][:], acc[GATE, b, s0], ACT.Sigmoid)

        def make_step(b, s0):
            step[b, s0] = values("step", b, s0)
            nc.vector.scalar_tensor_tensor(
                step[b, s0][:], acc[CANDIDATE, b, s0], 0.0, old[b, s0][:], ALU.max, ALU.subtract
            )

        def make_moves(b):
            for s0 in HALVES:
                move[b, s0] = values("move", b, s0)
                nc.vector.tensor_tensor(move[b, s0][:], step[b, s0][:], gate[b, s0][:], ALU.mult)

        fetch_old(0)
        make_gate(0, EARLY)
        make_step(0, EARLY)
        make_gate(0, LATE)
        make_step(0, LATE)
        fetch_old(1)
        for s0 in HALVES:
            make_gate(1, s0)
        make_moves(0)
        for s0, engine in ((EARLY, nc.vector), (LATE, nc.gpsimd)):
            new[s0] = values("new", 0, s0)
            engine.tensor_tensor(new[s0][:], move[0, s0][:], old[0, s0][:], ALU.add)
        for s0 in HALVES:
            make_step(1, s0)
        make_moves(1)

        for s0 in HALVES:
            nc.scalar.activation(window(0, s0), new[s0][:], ACT.Copy)
        nc.sync.dma_start(out=out[0:P, :], in_=memory[0][:])
        for s0 in HALVES:
            nc.vector.tensor_tensor(window(1, s0), move[1, s0][:], old[1, s0][:], ALU.add)
        nc.sync.dma_start(out=out[P : 2 * P, :], in_=memory[1][:])
